import numpy as np, ml_dtypes
CORES = [3,11,19,27,35,43,51,59]
N = 8
import mx_ref
BF = ml_dtypes.bfloat16
def cols(t, e):
    v = np.concatenate([t.reshape(128, -1, 4), np.zeros((128, 1, 4), BF)], axis=1)
    return np.ascontiguousarray(v[:, e]).reshape(128, -1)
def cut(t, i, w=512):
    return t[:, w * i:w * i + w]
def f(rng, *shape):
    return mx_ref.flush((rng.standard_normal(shape, dtype=np.float32) * np.exp2(rng.integers(-2, 3, shape[:-1] + (1,)))).astype(BF))
def wide(rng, *shape, cols=0):
    v = rng.standard_normal(shape, dtype=np.float32) * np.exp2(rng.integers(-12, 13, shape)).astype(np.float32)
    if cols: v *= np.repeat(np.exp2(rng.integers(-cols, cols + 1, shape[:-2] + (1, shape[-1] // 4))) * (rng.random(shape[:-2] + (1, shape[-1] // 4)) > 0.0625), 4, axis=-1).astype(np.float32)
    return mx_ref.flush(v.astype(BF))
WD, T, PL, CP, NC = 16, 256, 128, 16, 56
def scores(u, x):
    return np.stack([mx_ref.matmul(mx_ref.quantize(u[r]), mx_ref.quantize(x[r]))[0] for r in range(N)])
def fronts(P):
    a = np.zeros(P.shape, bool)
    v, h = P[1:] != P[:-1], P[:, 1:] != P[:, :-1]
    a[1:] |= v; a[:-1] |= v; a[:, 1:] |= h; a[:, :-1] |= h
    return a
def dealt(P):
    i, j = np.nonzero(fronts(P))
    g = np.full((16 * N + 2, WD + 2), -1)
    g[1:-1, 1:-1] = np.arange(N * T).reshape(16 * N, WD)
    n = np.arange(len(i)); D = np.full((N, PL, 5), -1)
    D[(n // 8) % N, 8 * (n // (8 * N)) + n % 8] = np.stack([g[i + 1, j + 1], g[i, j + 1], g[i + 2, j + 1], g[i + 1, j], g[i + 1, j + 2]], axis=1)
    return D
def needed(P):
    return np.stack([np.bincount(e[e >= 0] // T, minlength=N) for e in [np.unique(k) for k in dealt(P)]])
def broken(P):
    if np.sum(fronts(P)) > PL * N: return ["too many active cells"]
    b = []; D = dealt(P)
    for r in range(N):
        c, e = D[r, :, 0], np.unique(D[r])
        if np.bincount(c[c >= 0] // T, minlength=N).max() > CP: b.append("cells of one stripe dealt to one rank")
        if np.bincount(e[e >= 0] // T, minlength=N).max() > NC: b.append("columns of one stripe that one rank needs")
    return b
def smooth(rng, i):
    a, b = np.indices((16 * N, WD)); g = 0
    for _ in range(6):
        t, k, p = rng.uniform(-1, 1), 0.7 * 0.97 ** i * rng.uniform(0.7, 1.4), rng.uniform(0, 6.2832)
        g = g + np.cos(k * (np.cos(t) * a + np.sin(t) * b) + p)
    return g > 0
def straight(rng, i):
    a = np.indices((16 * N, WD))[0]
    return ((a + rng.integers(1, 4)) // 4) % 2 == 0
def islands(rng, i):
    at = [(0, 0), (15, WD // 2)]
    for c in rng.permutation(N * T):
        if len(at) >= int(N * T * 0.0625 * 0.98 ** i): break
        p, q = divmod(int(c), WD)
        if all(abs(p - a) + abs(q - b) >= 3 for a, b in at): at.append((p, q))
    P = np.zeros((16 * N, WD), bool)
    for p, q in at: P[p, q] = True
    return P
def few(rng, i):
    gone = [int(q) for q in 1 + rng.permutation(N - 1)[:rng.integers(1, 3)]]
    if len(gone) == 2 and abs(gone[0] - gone[1]) == 1: gone.pop()
    here = [q for q in range(N) if q not in gone]
    free = [q for q in here if q - 1 not in gone and q + 1 not in gone]
    P = np.zeros((16 * N, WD), bool)
    for q in here:
        if q - 1 in gone: P[16 * q + 1, rng.integers(0, WD)] = True
        if q + 1 in gone: P[16 * q + 14, rng.integers(0, WD)] = True
    for q in free + here[:rng.integers(0, 2)]: P[16 * q + rng.integers(1, 16 if q + 1 in here else 15), rng.integers(0, WD)] = True
    return P
def heavy(rng, i):
    a, b = np.indices((16 * N, WD)); n = np.zeros(a.shape, int); most = rng.integers(0, N)
    low = b % 2 == 1 if WD == 8 else ((b % 2 == 0) & (b > 0)) | (b == WD - 1)
    for r in range(N):
        if r == most:
            for k in (6, 10): n += a >= 16 * r + k + low
            n += a >= 16 * r + 14
            if WD == 8: n[16 * r + 2, 0] += 1
            else: n += a >= 16 * r + 2
        else:
            w = rng.integers(5, 12) + max(0, 3 - 0.1 * i) * np.sin(rng.uniform(0.2, 0.8) * np.arange(WD) + rng.uniform(0, 6.2832))
            n += a >= 16 * r + np.clip(np.rint(w), 2, 14)[None, :]
    return n % 2 == 0
def borders(rng, i):
    a, b = np.indices((16 * N, WD))
    return (a // 16 + (b < rng.integers(1, WD))) % 2 == 0
def drawn(rng, make, uneven=False, idle=False):
    for i in range(50):
        P = make(rng, i) ^ bool(rng.integers(0, 2))
        c = fronts(P).reshape(N, T).sum(axis=1)
        if c.sum() < (1 if idle else 8 * N) or broken(P): continue
        m = needed(P) * (1 - np.eye(N, dtype=int))
        if uneven and (c.max() < 3 * c.min() or m.max() != NC): continue
        if idle and not 1 <= (c == 0).sum() <= 2: continue
        if idle and (c.sum() > 8 * (N - 1) or (c.sum() - 1) % 8 < 3): continue
        if idle and not (m.sum(axis=0)[c == 0] > 0).all(): continue
        return P
    raise RuntimeError("no field in 50 tries")
def sized(t):
    v = t.astype(np.float32)
    return np.where(np.abs(v) < 2.0 ** -30, np.float32(0), v).astype(BF)
def plant(rng, P, spread=False):
    u = sized(f(rng, 128, 512)); qu = mx_ref.quantize(u)
    x = np.zeros((N, 128, T, 4), BF); want = P.reshape(N, T)
    for r in range(N):
        left = np.arange(T)
        for i in range(50):
            k = len(left); m = 8 * -(-k // 8)
            t = sized(wide(rng, 128, 4 * m, cols=2) if spread else f(rng, 128, 4 * m))
            s = mx_ref.matmul(qu, mx_ref.quantize(t))[0][:k]
            turn = np.where((s > 0) == want[r, left], 1, -1)
            t = (t.astype(np.float32).reshape(128, m, 4)[:, :k] * turn[None, :, None]).astype(BF)
            ok = np.abs(s) > 32
            x[r][:, left[ok]] = t[:, ok]
            left = left[~ok]
            if len(left) == 0: break
        else: raise RuntimeError("scores too small in 50 tries")
    return {"x": x.reshape(N, 128, 4 * T), "u": np.stack([u] * N), "w": sized(f(rng, N, 128, 5120))}
def setup_inputs(rng):
    return plant(rng, drawn(rng, smooth))
def setup_inputs_few(rng):
    return plant(rng, drawn(rng, few, idle=True))
def setup_inputs_near(rng):
    for i in range(50):
        d = plant(rng, drawn(rng, borders))
        s = scores(d["u"], d["x"])
        e = 1 + int(np.floor(np.log2(float(np.abs(s).min()))))
        d["u"] = sized((d["u"].astype(np.float32) * np.float32(2.0 ** -e)).astype(BF))
        t = scores(d["u"], d["x"])
        if 0.5 < np.abs(t).min() <= 1 and np.array_equal(t > 0, s > 0): return d
    raise RuntimeError("no scores near 0.5 in 50 tries")
def setup_inputs_spread(rng):
    return plant(rng, drawn(rng, islands), spread=True)
def setup_inputs_straight(rng):
    return plant(rng, drawn(rng, straight))
def setup_inputs_uneven(rng):
    return plant(rng, drawn(rng, heavy, uneven=True))
def check_inputs(d):
    b = []
    for k in ("x", "u", "w"):
        v = np.abs(d[k].astype(np.float32))
        if not ((v == 0) | ((v >= 2.0 ** -30) & (v <= 2.0 ** 30))).all(): b.append("sizes of " + k)
    if b: return b
    for r in range(N):
        if not np.array_equal(d["u"][r].astype(np.float32), d["u"][0].astype(np.float32)): b.append("u")
    s = scores(d["u"], d["x"])
    if not (np.abs(s) > 0.5).all(): b.append("score")
    return b + broken((s > 0).reshape(16 * N, WD))
def reference(x, u, w):
    P = (scores(u, x) > 0).reshape(16 * N, WD)
    D = dealt(P)
    m = max(8, 8 * -(-int(np.sum(fronts(P))) // (8 * N)))
    X = np.concatenate(list(x), axis=1)
    y = np.zeros((N, 128, 2 * PL), np.float32)
    for r in range(N):
        for k in range(5):
            q = mx_ref.quantize(cols(X, D[r, :m, k]))
            for o in range(2): y[r][:, PL * o:PL * o + m] += mx_ref.matmul(mx_ref.quantize(cut(w[r], 2 * k + o)), q)
    return {"y": y}

@@ -1,0 +1,433 @@
+from concourse.bass import DstId, RemoteDMATransfer
+from concourse.mybir import dt, AluOpType, ActivationFunctionType, AxisListType
+
+N = 8
+NC = 56
+Z0 = 16
+LW = Z0 + 64 * N
+
+SCRATCH = {
+    "aF": ("sbuf", [128, 10240], "float32"),
+    "aH": ("sbuf", [128, 5120], "bfloat16"),
+    "aI": ("sbuf", [128, 768], "int32"),
+    "aU": ("sbuf", [128, 512], "uint16"),
+    "sg": ("sbuf", [128, 128], "bfloat16"),
+    "xt": ("sbuf", [128, 1024], "bfloat16"),
+    "ut": ("sbuf", [128, 512], "bfloat16"),
+    "wt": ("sbuf", [128, 5120], "bfloat16"),
+    "zt": ("sbuf", [128, 512], "bfloat16"),
+    "xq": ("sbuf", [128, 256], "float8_e4m3fn_x4"),
+    "xs": ("sbuf", [128, 256], "uint8"),
+    "uq": ("sbuf", [128, 128], "float8_e4m3fn_x4"),
+    "us": ("sbuf", [128, 128], "uint8"),
+    "rq": ("sbuf", [128, 128], "float8_e4m3fn_x4"),
+    "rs": ("sbuf", [128, 128], "uint8"),
+    "wq": ("sbuf", [128, 1280], "float8_e4m3fn_x4"),
+    "ws": ("sbuf", [128, 1280], "uint8"),
+    "zq": ("sbuf", [128, 128], "float8_e4m3fn_x4"),
+    "zs": ("sbuf", [128, 128], "uint8"),
+    "slq": ("sbuf", [128, 512], "float8_e4m3fn_x4"),
+    "sls": ("sbuf", [128, 512], "uint8"),
+    "laq": ("sbuf", [128, LW], "float8_e4m3fn_x4"),
+    "las": ("sbuf", [128, LW], "uint8"),
+    "tq": ("sbuf", [128, 640], "float8_e4m3fn_x4"),
+    "ts": ("sbuf", [128, 640], "uint8"),
+    "yo": ("sbuf", [128, 256], "float32"),
+    "ps": ("psum", [128, 2048], "float32"),
+}
+DMAS = ["dx0", "dx1", "du", "dw0", "dw1", "dw2", "dz0", "dz1", "dy0", "dy1"]
+SEMAPHORES = ["qv", "qs", "qt", "qg"] + DMAS + ["rsign", "lsign", "rland", "lland"]
+
+A = AluOpType
+AF = ActivationFunctionType
+AX = AxisListType.X
+MUL, ADD, SUB, MAX, MIN = A.mult, A.add, A.subtract, A.max, A.min
+EQ, NE, LT, GE = A.is_equal, A.not_equal, A.is_lt, A.is_ge
+
+
+def rank_program(g, core, T, topo):
+    r = T.rank_of(core)
+    if r is None:
+        return
+    queues = {"v": g.vector, "s": g.scalar, "t": g.tensor, "g": g, "y": g.sync}
+    csem = {"v": "qv", "s": "qs", "t": "qt", "g": "qg"}
+    count = {}
+    known = {q: {} for q in queues}
+    hist = {}
+    used = {"aF": 0, "aH": 0, "aI": 0, "aU": 0}
+    unit = {"aF": 8, "aH": 16, "aI": 8, "aU": 16}
+
+    def V(name, a, b, p=0, e=128, step=1):
+        return (name, a, b, p, e, step)
+
+    def new(arena, n):
+        a = used[arena]
+        used[arena] = a + -(-n // unit[arena]) * unit[arena]
+        return V(arena, a, a + n)
+
+    def sub(v, a, b, step=1, p=0, e=128):
+        return V(v[0], v[1] + a, v[1] + b, p, e, step)
+
+    def ap(v):
+        if v[3] == 0 and v[4] == 128:
+            return T[v[0]][:, v[1]:v[2]:v[5]] if v[5] != 1 else T[v[0]][:, v[1]:v[2]]
+        return T[v[0]][v[3]:v[4], v[1]:v[2]:v[5]] if v[5] != 1 else T[v[0]][v[3]:v[4], v[1]:v[2]]
+
+    def note(v, write, q, sem, val, clock):
+        hist.setdefault(v[0], []).append((v, write, q, sem, val, clock))
+
+    def sync(q, outs, ins):
+        need = {}
+        for group, out in ((outs, True), (ins, False)):
+            for v in group:
+                for (o, write, oq, sem, val, clock) in hist.get(v[0], []):
+                    if not (write or out) or o[1] >= v[2] or v[1] >= o[2] or o[3] >= v[4] or v[3] >= o[4]:
+                        continue
+                    if not write and oq == q and sem == csem.get(q):
+                        continue
+                    if val > need.get(sem, (0, None))[0]:
+                        need[sem] = (val, clock)
+        mine = csem.get(q)
+        for sem in sorted(need, key=lambda s: (s == mine, s in DMAS, s)):
+            val, clock = need[sem]
+            if known[q].get(sem, 0) >= val:
+                continue
+            queues[q].wait_ge(T.sem[sem], val)
+            for s2, v2 in list(clock.items()) + [(sem, val)]:
+                known[q][s2] = max(known[q].get(s2, 0), v2)
+
+    def run(q, outs, ins, call, sem=None, n=1):
+        sync(q, outs, ins)
+        sem = sem or csem[q]
+        count[sem] = count.get(sem, 0) + n
+        call(queues[q]).then_inc(T.sem[sem], n)
+        clock = dict(known[q])
+        for v in outs:
+            note(v, True, q, sem, count[sem], clock)
+        for v in ins:
+            note(v, False, q, sem, count[sem], clock)
+
+    def sc(s, ins):
+        if isinstance(s, tuple):
+            ins.append(s)
+            return ap(s)
+        return s
+
+    def ts(o, i, s1, op0, s2=None, op1=None):
+        ins = [i]
+        a, b = sc(s1, ins), sc(s2, ins)
+        if op1 is None:
+            run("v", [o], ins, lambda e: e.tensor_scalar(ap(o), ap(i), a, None, op0))
+        else:
+            run("v", [o], ins, lambda e: e.tensor_scalar(ap(o), ap(i), a, b, op0, op1))
+        return o
+
+    def tt(o, a, b, op):
+        run("v", [o], [a, b], lambda e: e.tensor_tensor(ap(o), ap(a), ap(b), op))
+        return o
+
+    def cp(o, i):
+        run("v", [o], [i], lambda e: e.tensor_copy(ap(o), ap(i)))
+        return o
+
+    def tr(o, i):
+        run("v", [o], [i], lambda e: e.transpose(ap(o), ap(i)))
+        return o
+
+    def scan(o, d0, d1, init=0.0):
+        ins = [d0, d1]
+        s = sc(init, ins)
+        run("v", [o], ins, lambda e: e.tensor_tensor_scan(ap(o), ap(d0), ap(d1), s, MUL, ADD))
+        return o
+
+    def fill(o, c):
+        run("v", [o], [], lambda e: e.memset(ap(o), c))
+        return o
+
+    def total(o, i):
+        run("v", [o], [i], lambda e: e.tensor_reduce(ap(o), ap(i), AX, ADD))
+        return o
+
+    def gather(o, win, off):
+        run("v", [o], [win, off], lambda e: e.tensor_copy(ap(o), ap(win).indirect(ap(off))))
+        return o
+
+    def act(o, i, func, scale=1.0, bias=0.0, accum=None):
+        ins, outs = [i], [o]
+        a, b = sc(scale, ins), sc(bias, ins)
+        if accum is not None:
+            outs.append(accum)
+            run("s", outs, ins, lambda e: e.activation(ap(o), ap(i), func, bias=b, scale=a, accum_out=ap(accum)))
+        else:
+            run("s", outs, ins, lambda e: e.activation(ap(o), ap(i), func, bias=b, scale=a))
+        return o
+
+    def iota(o, pattern, base=0, lane=0):
+        run("g", [o], [], lambda e: e.iota(ap(o), pattern, base, lane, allow_small_or_imprecise_dtypes=o[0] != "aI"))
+        return o
+
+    def dma(q, o, i, sem, bits=False):
+        def call(e):
+            a = ap(o) if isinstance(o, tuple) else o
+            b = ap(i) if isinstance(i, tuple) else i
+            return e.dma_start(a.bitcast(dt.uint8), b.bitcast(dt.uint8)) if bits else e.dma_start(a, b)
+        run(q, [v for v in (o,) if isinstance(v, tuple)], [v for v in (i,) if isinstance(v, tuple)], call, sem, 16)
+
+    def quant(q, s, i):
+        run("v", [q, s], [i], lambda e: e.quantize_mx(ap(q), ap(s), ap(i)))
+
+    def pick(cq, cs, wq, ws, off):
+        run("v", [cq], [wq, off], lambda e: e.tensor_copy(ap(cq).bitcast(dt.uint32), ap(wq).bitcast(dt.uint32).indirect(ap(off))))
+        run("s", [cs], [ws, off], lambda e: e.activation(ap(cs), ap(ws).indirect(ap(off)), AF.Copy))
+
+    def mm(o, wq, ws, xq, xs, start, stop):
+        run("t", [o] if start else [], [wq, ws, xq, xs], lambda e: e.matmul_mx(ap(o), ap(wq), ap(ws), ap(xq), ap(xs), start, stop))
+        if not start:
+            note(o, True, "t", "qt", count["qt"], dict(known["t"]))
+
+    others = [d for d in range(N) if d != r]
+
+    def send(pairs, bits, rsem, lsem, ins):
+        sync("g", [], ins)
+        xs = []
+        for k, (d, src, dst) in enumerate(pairs):
+            to = T.cores[d]
+            rid, pid, _ = topo.addr(to)
+            a, b = ap(src), ap(dst)
+            if bits:
+                a, b = a.bitcast(dt.uint8), b.bitcast(dt.uint8)
+            xs.append(RemoteDMATransfer(dst_ids=[DstId(rid=rid, pnc=pid)], dma_engine_mask=1 << topo.engines(core, to)[k],
+                                        remote_sem=T.sem[rsem], src=a, dst=b))
+        g.remote_dma_fused(xs, local_sem=T.sem[lsem])
+        count[lsem] = count.get(lsem, 0) + len(xs)
+        count[rsem] = count.get(rsem, 0) + len(xs)
+
+    dma("s", V("ut", 0, 512), T.u[:, 0:512], "du")
+    dma("y", V("xt", 0, 512), T.x[:, 0:512], "dx0")
+    dma("s", V("xt", 512, 1024), T.x[:, 512:1024], "dx1")
+    for k, (a, b) in enumerate(((0, 2048), (2048, 4096), (4096, 5120))):
+        dma("y", V("wt", a, b), T.w[:, a:b], "dw%d" % k)
+
+    lane = iota(new("aI", 1), [[0, 1]], 0, 1)
+    jj = iota(new("aF", 16), [[1, 16]])
+    F1 = lambda: new("aF", 1)
+    zero = fill(new("aU", 8), 0)
+    bF = cp(F1(), ts(new("aI", 1), lane, 31, A.bitwise_and))
+    lo = ts(F1(), bF, 16.0, LT)
+    hi = ts(F1(), bF, 16.0, GE)
+    j = tt(F1(), tt(F1(), ts(F1(), bF, -2.0, MUL, 31.0, ADD), hi, MUL), bF, ADD)
+    c0 = tt(F1(), ts(F1(), j, 15.0, EQ, 0.0625, MUL), ts(F1(), j, 0.0, NE, 0.0625, MUL), ADD)
+    c1 = ts(F1(), ts(F1(), j, 0.0, EQ, -8.0, MUL), 16.0, ADD)
+    d = ts(new("aF", 16), jj, j, SUB)
+    f1 = ts(new("aF", 16), d, 0.0, EQ, c0, MUL)
+    f2 = ts(new("aF", 16), d, 1.0, EQ, c1, MUL)
+    f3 = ts(new("aF", 16), d, 2.0, EQ, 1024.0, MUL)
+    f4 = ts(new("aF", 16), d, 3.0, GE)
+    f12 = tt(new("aF", 16), f1, f2, ADD)
+    f34 = tt(new("aF", 16), f3, f4, ADD)
+    ft = new("aF", 256)
+    tt(sub(ft, 0, 16), f12, f34, ADD)
+    for n in (16, 32, 64, 128):
+        cp(sub(ft, n, 2 * n), sub(ft, 0, n))
+    n1 = ts(F1(), j, 0.0, EQ, 2.0 / 1024, MUL)
+    n2 = ts(F1(), j, 13.5, LT, 2.0 / 1024, MUL)
+    n3 = ts(F1(), j, 14.0, EQ, 2.0, MUL)
+    n4 = ts(F1(), j, 15.0, EQ, 32.0, MUL)
+    nrm = tt(F1(), tt(F1(), n1, n2, ADD), tt(F1(), n3, n4, ADD), ADD)
+
+    quant(V("uq", 0, 128), V("us", 0, 128), V("ut", 0, 512))
+    pick(V("rq", 0, 128), V("rs", 0, 128), V("uq", 0, 128), V("us", 0, 128), zero)
+    sgn = new("aF", 256)
+    for h in (0, 1):
+        quant(V("xq", 128 * h, 128 * h + 128), V("xs", 128 * h, 128 * h + 128), V("xt", 512 * h, 512 * h + 512))
+        mm(V("ps", 512 * h, 512 * h + 128), V("rq", 0, 128), V("rs", 0, 128),
+           V("xq", 128 * h, 128 * h + 128), V("xs", 128 * h, 128 * h + 128), True, True)
+    for h in (0, 1):
+        ts(sub(sgn, 128 * h, 128 * h + 128), V("ps", 512 * h, 512 * h + 128), 0.0, A.is_gt, -0.5, ADD)
+    cells = scan(new("aF", 256), ft, sgn)
+    own = V("sg", 16 * r, 16 * r + 16)
+    ts(own, sub(cells, 15, 256, 16), nrm, MUL)
+    send([(k, own, own) for k in others], False, "rsign", "lsign", [own])
+    for k in others:
+        note(V("sg", 16 * k, 16 * k + 16), True, None, "rsign", count["rsign"], {})
+
+    b32 = iota(new("aF", 128), [[0, 4], [1, 32]])
+    t_y = iota(new("aF", 6), [[1, 3], [0, 2]], 16 * r)
+    t_tr = iota(new("aF", 16), [[-1, 16]], 79)
+    val = iota(new("aH", 256), [[-1, 16], [16, 16]], 15)
+    t_d = iota(new("aF", 8), [[16, 4], [0, 2]])
+    t_g = iota(new("aF", 8), [[32, 4], [0, 2]])
+    b16 = iota(new("aF", 256), [[0, 16], [1, 16]])
+    t_nb = iota(new("aF", 8), [[128, 8]], 8 * r)
+    np1 = iota(new("aF", 256), [[-128, 8], [0, 2], [-1, 16]], -(8 * r + 2))
+    np2 = iota(new("aF", 256), [[0, 16], [-56, 2], [0, 8]])
+    t_st = iota(new("aF", 128), [[64, 8], [0, 16]], Z0)
+
+    iF = cp(F1(), ts(new("aI", 1), lane, 15, A.bitwise_and))
+    gF = cp(F1(), ts(new("aI", 1), lane, 4, A.arith_shift_right))
+    i16 = ts(F1(), iF, 16.0, MUL)
+    ge = ts(F1(), gF, -8.0, MUL, float((1 << 20) + 56), ADD)
+    one0 = ts(F1(), bF, 0.0, EQ)
+    ones = fill(new("aH", 128), 1.0)
+    d0 = ts(new("aH", 128), ones, lo, MUL)
+    X = fill(new("aH", 130), 0.0)
+    M = fill(new("aH", 129), 1000.0)
+    off_y = ts(new("aU", 6), t_y, iF, ADD)
+    off_d = ts(new("aU", 8), t_d, iF, ADD)
+    trash = act(new("aF", 16), t_tr, AF.Identity, bias=i16)
+    rs = tt(new("aF", 128), ts(new("aF", 128), b32, 0.0, NE), ts(new("aF", 128), b32, 16.0, EQ, -2.0, MUL), ADD)
+    top = ts(F1(), hi, 16.0, MUL, 16.0, ADD)
+    mk = tt(new("aF", 32), ts(new("aF", 32), sub(b32, 0, 32), bF, GE), ts(new("aF", 32), sub(b32, 0, 32), top, LT), MUL)
+    win = fill(new("aH", 384), 0.0)
+    fill(V("zt", 0, 512), 0.0)
+    quant(V("zq", 0, 128), V("zs", 0, 128), V("zt", 0, 512))
+    dma("y", V("laq", 0, Z0), V("zq", 0, Z0), "dz0", True)
+    dma("y", V("las", 0, Z0), V("zs", 0, Z0), "dz1")
+    for a, b in ((0, 512), (512, 1024), (1024, 1280)):
+        quant(V("wq", a, b), V("ws", a, b), V("wt", 4 * a, 4 * b))
+    off_g = ts(new("aU", 8), t_g, iF, ADD)
+    off_t = ts(new("aU", 8), t_g, 15.0, ADD)
+    low8 = ts(F1(), iF, 7.5, A.is_gt, 56.0, MUL)
+    ln = ts(F1(), tt(F1(), low8, iF, ADD), 1.5, ADD)
+    nb = act(new("aF", 8), t_nb, AF.Identity, bias=ln)
+    npt = tt(new("aF", 256), np1, np2, ADD)
+    r16 = ts(new("aF", 256), b16, 0.0, NE)
+    dn = act(new("aF", 128), sub(r16, 0, 128), AF.Copy, scale=lo)
+    bt = act(new("aF", 128), tt(new("aF", 128), ts(new("aF", 128), sub(b16, 0, 128), 0.0, EQ), t_st, MUL), AF.Copy, scale=one0)
+    m0 = ts(F1(), lo, -1.0, MUL)
+    m1 = ts(F1(), hi, -1.0, MUL)
+    m2 = ts(F1(), hi, -1024.0, MUL)
+    hl = ts(F1(), iF, 14.5, LT, 1024.0, MUL)
+    hr = ts(F1(), iF, 0.5, A.is_gt, 2048.0, MUL)
+    m3 = tt(F1(), tt(F1(), hl, hr, ADD), lo, MUL)
+    tv = fill(new("aF", 129), 0.0)
+    pt = fill(new("aF", 129), 0.0)
+    pc = fill(new("aF", 130), 0.0)
+    ec = fill(new("aH", 130), 0.0)
+    E = fill(new("aH", 129), 0.0)
+
+    ab = act(new("aH", 128), V("sg", 0, 128), AF.Abs)
+    tt(sub(M, 1, 128), V("sg", 0, 127), V("sg", 1, 128), MUL)
+    v1 = tt(new("aH", 128), sub(M, 0, 128), sub(M, 1, 129), MIN)
+    v2 = tt(new("aH", 128), v1, ab, MIN)
+    av = ts(new("aH", 128), v2, 17.0, LT)
+    scan(sub(X, 1, 129), d0, av, one0)
+
+    Y = gather(new("aH", 96), X, off_y)
+    YT = tr(new("aH", 96), Y)
+    S6 = scan(new("aF", 96), sub(rs, 0, 96), YT)
+    V6 = tt(new("aI", 96), S6, YT, MUL)
+    A6 = ts(new("aI", 96), V6, 56 | 1 << 20, A.bitwise_and)
+    E6 = ts(new("aH", 96), A6, ge, EQ)
+    a1 = tt(new("aH", 16), sub(E6, 16, 32), sub(E6, 80, 96), MAX)
+    a2 = tt(new("aH", 16), sub(E6, 47, 63), sub(E6, 49, 65), MAX)
+    a3 = tt(new("aH", 16), a1, sub(E6, 48, 64), MAX)
+    nd = tt(new("aF", 16), a3, a2, MAX)
+    tot = total(F1(), nd)
+    pre = scan(new("aF", 16), sub(ones, 0, 16), nd)
+    mt = ts(new("aF", 32), mk, tot, MUL)
+    q2 = tt(new("aF", 16), nd, trash, MUL)
+    mtt = tr(new("aF", 32), mt)
+    q1 = tt(new("aF", 16), trash, pre, SUB)
+    base = total(F1(), mtt)
+    q3 = tt(new("aF", 16), q1, q2, SUB)
+    off = ts(new("aU", 16), q3, base, ADD)
+    run("v", [win], [off, val], lambda e: e.tensor_copy(ap(win).indirect(ap(off)), ap(val)))
+    D = gather(new("aH", 128), sub(win, 0, 64), off_d)
+    DT = tr(new("aH", 128), D)
+    lc = new("aH", 32)
+    for a in range(4):
+        for h in (0, 1):
+            o = sub(lc, 8 * a + 4 * h, 8 * a + 4 * h + 4, 1, 0, 32)
+            i = sub(DT, 16 * h, 128, 32, 32 * a, 32 * a + 32)
+            if a % 2:
+                run("s", [o], [i], lambda e: e.activation(ap(o), ap(i), AF.Copy))
+            else:
+                cp(o, i)
+    cp(sub(lc, 0, 32, 1, 32, 64), sub(lc, 0, 32, 1, 0, 32))
+    lw = new("aU", 32)
+    cp(sub(lw, 0, 32, 1, 0, 64), sub(lc, 0, 32, 1, 0, 64))
+    cp(sub(lw, 0, 32, 1, 64, 128), sub(lc, 0, 32, 1, 0, 64))
+
+    xq, xs = V("xq", 0, 256), V("xs", 0, 256)
+    for a, b in ((0, r), (r + 1, N)):
+        if a < b:
+            pick(V("slq", 64 * a, 64 * b), V("sls", 64 * a, 64 * b), xq, xs, sub(lw, 4 * a, 4 * b))
+    home = lambda n: V(n, Z0 + 64 * r, Z0 + 64 * r + NC)
+    send([(k, V("slq", 64 * k, 64 * k + NC), home("laq")) for k in others], True, "rland", "lland",
+         [V("slq", 64 * k, 64 * k + NC) for k in others])
+    send([(k, V("sls", 64 * k, 64 * k + NC), home("las")) for k in others], False, "rland", "lland",
+         [V("sls", 64 * k, 64 * k + NC) for k in others])
+    for k in others:
+        for n in ("laq", "las"):
+            note(V(n, Z0 + 64 * k, Z0 + 64 * k + NC), True, None, "rland", count["rland"], {})
+
+    ZR = tr(new("aH", 128), sub(X, 1, 129))
+    SR = scan(new("aF", 128), rs, ZR)
+    TG = gather(new("aF", 128), SR, off_t)
+    TF = tr(new("aF", 128), TG)
+    acc = new("aF", 8)
+    for c in range(8):
+        act(new("aH", 128), TF, AF.Sign, -1.0, sub(nb, c, c + 1), sub(acc, c, c + 1))
+    pick(V("laq", Z0 + 64 * r, Z0 + 64 * r + 64), V("las", Z0 + 64 * r, Z0 + 64 * r + 64), xq, xs, sub(lw, 4 * r, 4 * r + 4))
+    VR = tt(new("aI", 128), SR, ZR, MUL)
+    AR = ts(new("aI", 128), VR, 56 | 1 << 20, A.bitwise_and)
+    ts(sub(E, 0, 128), AR, float((1 << 20) + 56 - 8 * r), EQ)
+    H1 = tt(new("aH", 127), sub(E, 0, 127), sub(E, 2, 129), MAX)
+    w1 = tt(new("aF", 128), VR, sub(E, 0, 128), MUL)
+    H2 = tt(new("aH", 127), H1, sub(E, 1, 128), MAX)
+    w2 = new("aF", 128)
+    tt(sub(w2, 1, 128), sub(w1, 1, 128), H2, SUB)
+    wd = gather(new("aF", 128), sub(w2, 16, 128), off_g)
+    tr(sub(tv, 0, 128), wd)
+    ts(sub(ec, 1, 129), sub(tv, 0, 128), -1.5, LT)
+    nh = ts(new("aH", 128), sub(tv, 0, 128), -0.5, LT)
+    h1 = tt(new("aH", 128), sub(ec, 0, 128), sub(ec, 2, 130), MAX)
+    h2 = tt(new("aH", 128), h1, nh, MAX)
+    h3 = tt(new("aF", 128), h2, bt, ADD)
+    xn = scan(new("aF", 128), dn, h3)
+    zn = tr(new("aF", 128), xn)
+    sn = scan(new("aF", 128), rs, zn)
+    pd = gather(new("aF", 128), sub(sn, 16, 128), off_g)
+    tr(sub(pc, 1, 129), pd)
+    p1 = act(new("aF", 128), sub(pc, 1, 129), AF.Identity, m0, m3)
+    p2 = act(new("aF", 128), sub(pc, 0, 128), AF.Copy, m1)
+    p3 = ts(new("aF", 128), sub(pc, 2, 130), m2, MUL)
+    rp = new("aU", 16)
+    ts(sub(rp, 0, 16, 2), acc, 0.5, MUL, 64.0, ADD)
+    ts(sub(rp, 1, 16, 2), acc, 0.5, MUL, 64.0, ADD)
+    ov = gather(new("aF", 256), tv, rp)
+    oh = tt(new("aF", 256), ov, npt, EQ)
+    p4 = tt(new("aF", 128), p1, p3, ADD)
+    tt(sub(pt, 0, 128), p4, p2, ADD)
+    gp = gather(new("aF", 256), pt, rp)
+    op = tt(new("aF", 256), oh, gp, MUL)
+    ot = tr(new("aF", 256), op)
+    os_ = scan(new("aF", 256), r16, ot)
+    ai = cp(new("aI", 8), sub(os_, 15, 256, 32))
+    bi = cp(new("aI", 8), sub(os_, 31, 256, 32))
+    li = new("aI", 40)
+    k0 = ts(sub(li, 0, 8), ai, 1023, A.bitwise_and)
+    ts(sub(li, 8, 16), bi, 1023, A.bitwise_and)
+    ts(sub(li, 16, 24), bi, 10, A.arith_shift_right)
+    fl = ts(new("aI", 8), ai, 10, A.arith_shift_right, 1, A.bitwise_and)
+    fr = ts(new("aI", 8), ai, 11, A.arith_shift_right)
+    kl = ts(new("aI", 8), k0, -1.0, ADD)
+    kr = ts(new("aI", 8), k0, 1.0, ADD)
+    tt(sub(li, 24, 32), kl, fl, MUL)
+    tt(sub(li, 32, 40), kr, fr, MUL)
+    lu = cp(new("aU", 40), li)
+
+    for k in range(5):
+        pick(V("tq", 128 * k, 128 * k + 128), V("ts", 128 * k, 128 * k + 128), V("laq", 0, LW), V("las", 0, LW), sub(lu, 8 * k, 8 * k + 8))
+        for o in (0, 1):
+            a = 128 * (2 * k + o)
+            mm(V("ps", 1024 + 512 * o, 1152 + 512 * o), V("wq", a, a + 128), V("ws", a, a + 128),
+               V("tq", 128 * k, 128 * k + 128), V("ts", 128 * k, 128 * k + 128), k == 0, k == 4)
+    cp(V("yo", 0, 128), V("ps", 1024, 1152))
+    act(V("yo", 128, 256), V("ps", 1536, 1664), AF.Copy)
+    dma("y", T.y[:, 0:128], V("yo", 0, 128), "dy0")
+    dma("s", T.y[:, 128:256], V("yo", 128, 256), "dy1")
+    for sem in SEMAPHORES:
+        if count.get(sem, 0) > known["g"].get(sem, 0):
+            g.wait_ge(T.sem[sem], count[sem])

@@ -5,39 +5,16 @@ N = 8
 NC = 56
 Z0 = 16
 LW = Z0 + 64 * N
-
-SCRATCH = {
-    "aF": ("sbuf", [128, 10240], "float32"),
-    "aH": ("sbuf", [128, 5120], "bfloat16"),
-    "aI": ("sbuf", [128, 768], "int32"),
-    "aU": ("sbuf", [128, 512], "uint16"),
-    "sg": ("sbuf", [128, 128], "bfloat16"),
-    "xt": ("sbuf", [128, 1024], "bfloat16"),
-    "ut": ("sbuf", [128, 512], "bfloat16"),
-    "wt": ("sbuf", [128, 5120], "bfloat16"),
-    "zt": ("sbuf", [128, 512], "bfloat16"),
-    "xq": ("sbuf", [128, 256], "float8_e4m3fn_x4"),
-    "xs": ("sbuf", [128, 256], "uint8"),
-    "uq": ("sbuf", [128, 128], "float8_e4m3fn_x4"),
-    "us": ("sbuf", [128, 128], "uint8"),
-    "rq": ("sbuf", [128, 128], "float8_e4m3fn_x4"),
-    "rs": ("sbuf", [128, 128], "uint8"),
-    "wq": ("sbuf", [128, 1280], "float8_e4m3fn_x4"),
-    "ws": ("sbuf", [128, 1280], "uint8"),
-    "zq": ("sbuf", [128, 128], "float8_e4m3fn_x4"),
-    "zs": ("sbuf", [128, 128], "uint8"),
-    "slq": ("sbuf", [128, 512], "float8_e4m3fn_x4"),
-    "sls": ("sbuf", [128, 512], "uint8"),
-    "laq": ("sbuf", [128, LW], "float8_e4m3fn_x4"),
-    "las": ("sbuf", [128, LW], "uint8"),
-    "tq": ("sbuf", [128, 640], "float8_e4m3fn_x4"),
-    "ts": ("sbuf", [128, 640], "uint8"),
-    "yo": ("sbuf", [128, 256], "float32"),
-    "ps": ("psum", [128, 2048], "float32"),
-}
+F8, U8, BF, F32 = "float8_e4m3fn_x4", "uint8", "bfloat16", "float32"
+SCRATCH = {"aF": ("sbuf", [128, 10240], F32), "aH": ("sbuf", [128, 5120], BF), "aI": ("sbuf", [128, 768], "int32"),
+           "aU": ("sbuf", [128, 512], "uint16"), "sg": ("sbuf", [128, 128], BF), "xt": ("sbuf", [128, 1024], BF),
+           "ut": ("sbuf", [128, 512], BF), "wt": ("sbuf", [128, 5120], BF), "zt": ("sbuf", [128, 512], BF),
+           "yo": ("sbuf", [128, 256], F32), "ps": ("psum", [128, 2048], F32)}
+for _n, _w in (("x", 256), ("u", 128), ("r", 128), ("w", 1280), ("z", 128), ("sl", 512), ("la", LW), ("t", 640)):
+    SCRATCH[_n + "q"] = ("sbuf", [128, _w], F8)
+    SCRATCH[_n + "s"] = ("sbuf", [128, _w], U8)
 DMAS = ["dx0", "dx1", "du", "dw0", "dw1", "dw2", "dz0", "dz1", "dy0", "dy1"]
-SEMAPHORES = ["qv", "qs", "qt", "qg"] + DMAS + ["rsign", "lsign", "rland", "lland"]
-
+SEMAPHORES = ["qv", "qs", "qt", "qg"] + DMAS + ["rsign", "lsign", "rlc", "rls", "lland"]
 A = AluOpType
 AF = ActivationFunctionType
 AX = AxisListType.X
@@ -148,8 +125,11 @@ def rank_program(g, core, T, topo):
         run("v", [o], [i], lambda e: e.tensor_reduce(ap(o), ap(i), AX, ADD))
         return o
 
-    def gather(o, win, off):
-        run("v", [o], [win, off], lambda e: e.tensor_copy(ap(o), ap(win).indirect(ap(off))))
+    def gather(o, win, off, q="v"):
+        if q == "v":
+            run("v", [o], [win, off], lambda e: e.tensor_copy(ap(o), ap(win).indirect(ap(off))))
+        else:
+            run("s", [o], [win, off], lambda e: e.activation(ap(o), ap(win).indirect(ap(off)), AF.Copy))
         return o
 
     def act(o, i, func, scale=1.0, bias=0.0, accum=None):
@@ -166,6 +146,13 @@ def rank_program(g, core, T, topo):
         run("g", [o], [], lambda e: e.iota(ap(o), pattern, base, lane, allow_small_or_imprecise_dtypes=o[0] != "aI"))
         return o
 
+    def const(o, c):
+        return iota(o, [[0, o[2] - o[1]]], c)
+
+    def asel(o, i, pattern, op, c, base):
+        run("g", [o], [i], lambda e: e.affine_select(ap(o), ap(i), pattern, op, c, base, 0))
+        return o
+
     def dma(q, o, i, sem, bits=False):
         def call(e):
             a = ap(o) if isinstance(o, tuple) else o
@@ -176,9 +163,8 @@ def rank_program(g, core, T, topo):
     def quant(q, s, i):
         run("v", [q, s], [i], lambda e: e.quantize_mx(ap(q), ap(s), ap(i)))
 
-    def pick(cq, cs, wq, ws, off):
+    def pickc(cq, wq, off):
         run("v", [cq], [wq, off], lambda e: e.tensor_copy(ap(cq).bitcast(dt.uint32), ap(wq).bitcast(dt.uint32).indirect(ap(off))))
-        run("s", [cs], [ws, off], lambda e: e.activation(ap(cs), ap(ws).indirect(ap(off)), AF.Copy))
 
     def mm(o, wq, ws, xq, xs, start, stop):
         run("t", [o] if start else [], [wq, ws, xq, xs], lambda e: e.matmul_mx(ap(o), ap(wq), ap(ws), ap(xq), ap(xs), start, stop))
@@ -210,6 +196,17 @@ def rank_program(g, core, T, topo):
 
     lane = iota(new("aI", 1), [[0, 1]], 0, 1)
     jj = iota(new("aF", 16), [[1, 16]])
+    bb = iota(new("aF", 32), [[1, 32]])
+    t_y = iota(new("aF", 6), [[1, 3], [0, 2]], 16 * r)
+    t_tr = iota(new("aF", 16), [[-1, 16]], 79)
+    t_d = iota(new("aF", 8), [[16, 4], [0, 2]])
+    t_g = iota(new("aF", 8), [[32, 4], [0, 2]])
+    ones = const(new("aH", 128), 1)
+    X, M = new("aH", 130), new("aH", 129)
+    const(sub(X, 0, 1), 0)
+    const(sub(X, 129, 130), 0)
+    const(sub(M, 0, 1), 1000)
+    const(sub(M, 128, 129), 1000)
     F1 = lambda: new("aF", 1)
     zero = fill(new("aU", 8), 0)
     bF = cp(F1(), ts(new("aI", 1), lane, 31, A.bitwise_and))
@@ -236,7 +233,8 @@ def rank_program(g, core, T, topo):
     nrm = tt(F1(), tt(F1(), n1, n2, ADD), tt(F1(), n3, n4, ADD), ADD)
 
     quant(V("uq", 0, 128), V("us", 0, 128), V("ut", 0, 512))
-    pick(V("rq", 0, 128), V("rs", 0, 128), V("uq", 0, 128), V("us", 0, 128), zero)
+    pickc(V("rq", 0, 128), V("uq", 0, 128), zero)
+    gather(V("rs", 0, 128), V("us", 0, 128), zero, "s")
     sgn = new("aF", 256)
     for h in (0, 1):
         quant(V("xq", 128 * h, 128 * h + 128), V("xs", 128 * h, 128 * h + 128), V("xt", 512 * h, 512 * h + 512))
@@ -251,60 +249,43 @@ def rank_program(g, core, T, topo):
     for k in others:
         note(V("sg", 16 * k, 16 * k + 16), True, None, "rsign", count["rsign"], {})
 
-    b32 = iota(new("aF", 128), [[0, 4], [1, 32]])
-    t_y = iota(new("aF", 6), [[1, 3], [0, 2]], 16 * r)
-    t_tr = iota(new("aF", 16), [[-1, 16]], 79)
+    onef = const(new("aF", 256), 1)
+    rs0 = asel(new("aF", 128), sub(onef, 0, 128), [[0, 4], [1, 32]], NE, 0.0, 0)
+    rs = asel(new("aF", 128), rs0, [[0, 4], [1, 32]], NE, -1.0, -16)
+    win = new("aH", 384)
+    const(sub(win, 0, 64), 0)
     val = iota(new("aH", 256), [[-1, 16], [16, 16]], 15)
-    t_d = iota(new("aF", 8), [[16, 4], [0, 2]])
-    t_g = iota(new("aF", 8), [[32, 4], [0, 2]])
-    b16 = iota(new("aF", 256), [[0, 16], [1, 16]])
+    tv, pt, pc, ec, E = new("aF", 129), new("aF", 129), new("aF", 130), new("aH", 130), new("aH", 129)
+    for v, a in ((E, 128), (ec, 0), (ec, 129), (tv, 128), (pc, 0), (pc, 129), (pt, 128)):
+        const(sub(v, a, a + 1), 0)
     t_nb = iota(new("aF", 8), [[128, 8]], 8 * r)
+    t_st = iota(new("aF", 128), [[64, 8], [0, 16]], Z0)
+    st0 = asel(new("aF", 128), t_st, [[0, 8], [1, 16]], EQ, 0.0, 0)
+    r16 = asel(new("aF", 256), onef, [[0, 16], [1, 16]], NE, 0.0, 0)
     np1 = iota(new("aF", 256), [[-128, 8], [0, 2], [-1, 16]], -(8 * r + 2))
     np2 = iota(new("aF", 256), [[0, 16], [-56, 2], [0, 8]])
-    t_st = iota(new("aF", 128), [[64, 8], [0, 16]], Z0)
 
+    d0 = act(new("aH", 128), ones, AF.Copy, scale=lo)
+    m0 = act(F1(), lo, AF.Copy, scale=-1.0)
+    m1 = act(F1(), hi, AF.Copy, scale=-1.0)
+    m2 = act(F1(), hi, AF.Copy, scale=-1024.0)
+    one0 = ts(F1(), bF, 0.0, EQ)
     iF = cp(F1(), ts(new("aI", 1), lane, 15, A.bitwise_and))
     gF = cp(F1(), ts(new("aI", 1), lane, 4, A.arith_shift_right))
-    i16 = ts(F1(), iF, 16.0, MUL)
-    ge = ts(F1(), gF, -8.0, MUL, float((1 << 20) + 56), ADD)
-    one0 = ts(F1(), bF, 0.0, EQ)
-    ones = fill(new("aH", 128), 1.0)
-    d0 = ts(new("aH", 128), ones, lo, MUL)
-    X = fill(new("aH", 130), 0.0)
-    M = fill(new("aH", 129), 1000.0)
     off_y = ts(new("aU", 6), t_y, iF, ADD)
     off_d = ts(new("aU", 8), t_d, iF, ADD)
+    i16 = ts(F1(), iF, 16.0, MUL)
+    ge = ts(F1(), gF, -8.0, MUL, float((1 << 20) + 56), ADD)
     trash = act(new("aF", 16), t_tr, AF.Identity, bias=i16)
-    rs = tt(new("aF", 128), ts(new("aF", 128), b32, 0.0, NE), ts(new("aF", 128), b32, 16.0, EQ, -2.0, MUL), ADD)
     top = ts(F1(), hi, 16.0, MUL, 16.0, ADD)
-    mk = tt(new("aF", 32), ts(new("aF", 32), sub(b32, 0, 32), bF, GE), ts(new("aF", 32), sub(b32, 0, 32), top, LT), MUL)
-    win = fill(new("aH", 384), 0.0)
+    mk1 = ts(new("aF", 32), bb, bF, GE)
+    mk2 = ts(new("aF", 32), bb, top, LT)
+    mk = tt(new("aF", 32), mk1, mk2, MUL)
     fill(V("zt", 0, 512), 0.0)
     quant(V("zq", 0, 128), V("zs", 0, 128), V("zt", 0, 512))
     dma("y", V("laq", 0, Z0), V("zq", 0, Z0), "dz0", True)
     dma("y", V("las", 0, Z0), V("zs", 0, Z0), "dz1")
-    for a, b in ((0, 512), (512, 1024), (1024, 1280)):
-        quant(V("wq", a, b), V("ws", a, b), V("wt", 4 * a, 4 * b))
-    off_g = ts(new("aU", 8), t_g, iF, ADD)
-    off_t = ts(new("aU", 8), t_g, 15.0, ADD)
-    low8 = ts(F1(), iF, 7.5, A.is_gt, 56.0, MUL)
-    ln = ts(F1(), tt(F1(), low8, iF, ADD), 1.5, ADD)
-    nb = act(new("aF", 8), t_nb, AF.Identity, bias=ln)
-    npt = tt(new("aF", 256), np1, np2, ADD)
-    r16 = ts(new("aF", 256), b16, 0.0, NE)
-    dn = act(new("aF", 128), sub(r16, 0, 128), AF.Copy, scale=lo)
-    bt = act(new("aF", 128), tt(new("aF", 128), ts(new("aF", 128), sub(b16, 0, 128), 0.0, EQ), t_st, MUL), AF.Copy, scale=one0)
-    m0 = ts(F1(), lo, -1.0, MUL)
-    m1 = ts(F1(), hi, -1.0, MUL)
-    m2 = ts(F1(), hi, -1024.0, MUL)
-    hl = ts(F1(), iF, 14.5, LT, 1024.0, MUL)
-    hr = ts(F1(), iF, 0.5, A.is_gt, 2048.0, MUL)
-    m3 = tt(F1(), tt(F1(), hl, hr, ADD), lo, MUL)
-    tv = fill(new("aF", 129), 0.0)
-    pt = fill(new("aF", 129), 0.0)
-    pc = fill(new("aF", 130), 0.0)
-    ec = fill(new("aH", 130), 0.0)
-    E = fill(new("aH", 129), 0.0)
+    quant(V("wq", 0, 512), V("ws", 0, 512), V("wt", 0, 2048))
 
     ab = act(new("aH", 128), V("sg", 0, 128), AF.Abs)
     tt(sub(M, 1, 128), V("sg", 0, 127), V("sg", 1, 128), MUL)
@@ -352,55 +333,67 @@ def rank_program(g, core, T, topo):
     xq, xs = V("xq", 0, 256), V("xs", 0, 256)
     for a, b in ((0, r), (r + 1, N)):
         if a < b:
-            pick(V("slq", 64 * a, 64 * b), V("sls", 64 * a, 64 * b), xq, xs, sub(lw, 4 * a, 4 * b))
+            pickc(V("slq", 64 * a, 64 * b), xq, sub(lw, 4 * a, 4 * b))
+            gather(V("sls", 64 * a, 64 * b), xs, sub(lw, 4 * a, 4 * b), "s")
     home = lambda n: V(n, Z0 + 64 * r, Z0 + 64 * r + NC)
-    send([(k, V("slq", 64 * k, 64 * k + NC), home("laq")) for k in others], True, "rland", "lland",
-         [V("slq", 64 * k, 64 * k + NC) for k in others])
-    send([(k, V("sls", 64 * k, 64 * k + NC), home("las")) for k in others], False, "rland", "lland",
-         [V("sls", 64 * k, 64 * k + NC) for k in others])
+    slot = lambda n, k: V(n, 64 * k, 64 * k + NC)
+    send([(k, slot("slq", k), home("laq")) for k in others], True, "rlc", "lland", [slot("slq", k) for k in others])
+    send([(k, slot("sls", k), home("las")) for k in others], False, "rls", "lland", [slot("sls", k) for k in others])
     for k in others:
-        for n in ("laq", "las"):
-            note(V(n, Z0 + 64 * k, Z0 + 64 * k + NC), True, None, "rland", count["rland"], {})
+        for n, m in (("laq", "rlc"), ("las", "rls")):
+            note(V(n, Z0 + 64 * k, Z0 + 64 * k + NC), True, None, m, count[m], {})
 
+    off_t = ts(new("aU", 8), t_g, 15.0, ADD)
     ZR = tr(new("aH", 128), sub(X, 1, 129))
     SR = scan(new("aF", 128), rs, ZR)
-    TG = gather(new("aF", 128), SR, off_t)
+    TG = gather(new("aF", 128), SR, off_t, "s")
+    low8 = ts(F1(), iF, 7.5, A.is_gt, 56.0, MUL)
+    VR = tt(new("aI", 128), SR, ZR, MUL)
+    ln = ts(F1(), tt(F1(), low8, iF, ADD), 1.5, ADD)
+    nb = act(new("aF", 8), t_nb, AF.Identity, bias=ln)
+    AR = ts(new("aI", 128), VR, 56 | 1 << 20, A.bitwise_and)
     TF = tr(new("aF", 128), TG)
     acc = new("aF", 8)
     for c in range(8):
         act(new("aH", 128), TF, AF.Sign, -1.0, sub(nb, c, c + 1), sub(acc, c, c + 1))
-    pick(V("laq", Z0 + 64 * r, Z0 + 64 * r + 64), V("las", Z0 + 64 * r, Z0 + 64 * r + 64), xq, xs, sub(lw, 4 * r, 4 * r + 4))
-    VR = tt(new("aI", 128), SR, ZR, MUL)
-    AR = ts(new("aI", 128), VR, 56 | 1 << 20, A.bitwise_and)
     ts(sub(E, 0, 128), AR, float((1 << 20) + 56 - 8 * r), EQ)
+    off_g = ts(new("aU", 8), t_g, iF, ADD)
+    hl = ts(F1(), iF, 14.5, LT, 1024.0, MUL)
     H1 = tt(new("aH", 127), sub(E, 0, 127), sub(E, 2, 129), MAX)
     w1 = tt(new("aF", 128), VR, sub(E, 0, 128), MUL)
     H2 = tt(new("aH", 127), H1, sub(E, 1, 128), MAX)
+    hr = ts(F1(), iF, 0.5, A.is_gt, 2048.0, MUL)
     w2 = new("aF", 128)
     tt(sub(w2, 1, 128), sub(w1, 1, 128), H2, SUB)
     wd = gather(new("aF", 128), sub(w2, 16, 128), off_g)
     tr(sub(tv, 0, 128), wd)
+    dn = act(new("aF", 128), sub(r16, 0, 128), AF.Copy, scale=lo)
+    bt = act(new("aF", 128), st0, AF.Copy, scale=one0)
     ts(sub(ec, 1, 129), sub(tv, 0, 128), -1.5, LT)
     nh = ts(new("aH", 128), sub(tv, 0, 128), -0.5, LT)
     h1 = tt(new("aH", 128), sub(ec, 0, 128), sub(ec, 2, 130), MAX)
     h2 = tt(new("aH", 128), h1, nh, MAX)
     h3 = tt(new("aF", 128), h2, bt, ADD)
+    rp = new("aU", 16)
+    ts(sub(rp, 0, 16, 2), acc, 0.5, MUL, 64.0, ADD)
+    ts(sub(rp, 1, 16, 2), acc, 0.5, MUL, 64.0, ADD)
+    ov = gather(new("aF", 256), tv, rp, "s")
     xn = scan(new("aF", 128), dn, h3)
     zn = tr(new("aF", 128), xn)
     sn = scan(new("aF", 128), rs, zn)
+    m3 = tt(F1(), tt(F1(), hl, hr, ADD), lo, MUL)
     pd = gather(new("aF", 128), sub(sn, 16, 128), off_g)
     tr(sub(pc, 1, 129), pd)
     p1 = act(new("aF", 128), sub(pc, 1, 129), AF.Identity, m0, m3)
     p2 = act(new("aF", 128), sub(pc, 0, 128), AF.Copy, m1)
     p3 = ts(new("aF", 128), sub(pc, 2, 130), m2, MUL)
-    rp = new("aU", 16)
-    ts(sub(rp, 0, 16, 2), acc, 0.5, MUL, 64.0, ADD)
-    ts(sub(rp, 1, 16, 2), acc, 0.5, MUL, 64.0, ADD)
-    ov = gather(new("aF", 256), tv, rp)
-    oh = tt(new("aF", 256), ov, npt, EQ)
+    npt = tt(new("aF", 256), np1, np2, ADD)
     p4 = tt(new("aF", 128), p1, p3, ADD)
     tt(sub(pt, 0, 128), p4, p2, ADD)
-    gp = gather(new("aF", 256), pt, rp)
+    gp = gather(new("aF", 256), pt, rp, "s")
+    oh = tt(new("aF", 256), ov, npt, EQ)
+    pickc(V("laq", Z0 + 64 * r, Z0 + 64 * r + 64), xq, sub(lw, 4 * r, 4 * r + 4))
+    gather(V("las", Z0 + 64 * r, Z0 + 64 * r + 64), xs, sub(lw, 4 * r, 4 * r + 4), "s")
     op = tt(new("aF", 256), oh, gp, MUL)
     ot = tr(new("aF", 256), op)
     os_ = scan(new("aF", 256), r16, ot)
@@ -417,13 +410,19 @@ def rank_program(g, core, T, topo):
     tt(sub(li, 24, 32), kl, fl, MUL)
     tt(sub(li, 32, 40), kr, fr, MUL)
     lu = cp(new("aU", 40), li)
+    for a, b in ((512, 1024), (1024, 1280)):
+        quant(V("wq", a, b), V("ws", a, b), V("wt", 4 * a, 4 * b))
 
+    tk = lambda n, k: V(n, 128 * k, 128 * k + 128)
+    lk = lambda k: sub(lu, 8 * k, 8 * k + 8)
     for k in range(5):
-        pick(V("tq", 128 * k, 128 * k + 128), V("ts", 128 * k, 128 * k + 128), V("laq", 0, LW), V("las", 0, LW), sub(lu, 8 * k, 8 * k + 8))
+        pickc(tk("tq", k), V("laq", 0, LW), lk(k))
+    for k in (0, 3, 1, 4, 2):
+        gather(tk("ts", k), V("las", 0, LW), lk(k), "v" if k > 2 else "s")
+    for k in (0, 3, 1, 4, 2):
         for o in (0, 1):
             a = 128 * (2 * k + o)
-            mm(V("ps", 1024 + 512 * o, 1152 + 512 * o), V("wq", a, a + 128), V("ws", a, a + 128),
-               V("tq", 128 * k, 128 * k + 128), V("ts", 128 * k, 128 * k + 128), k == 0, k == 4)
+            mm(V("ps", 1024 + 512 * o, 1152 + 512 * o), V("wq", a, a + 128), V("ws", a, a + 128), tk("tq", k), tk("ts", k), k == 0, k == 2)
     cp(V("yo", 0, 128), V("ps", 1024, 1152))
     act(V("yo", 128, 256), V("ps", 1536, 1664), AF.Copy)
     dma("y", T.y[:, 0:128], V("yo", 0, 128), "dy0")

@@ -188,19 +188,21 @@ def rank_program(g, core, T, topo):
         count[lsem] = count.get(lsem, 0) + len(xs)
         count[rsem] = count.get(rsem, 0) + len(xs)
 
-    dma("s", V("ut", 0, 512), T.u[:, 0:512], "du")
+    dma("s", V("ut", 0, 8), T.u[:, 0:8], "du")
     dma("y", V("xt", 0, 512), T.x[:, 0:512], "dx0")
     dma("s", V("xt", 512, 1024), T.x[:, 512:1024], "dx1")
     for k, (a, b) in enumerate(((0, 2048), (2048, 4096), (4096, 5120))):
         dma("y", V("wt", a, b), T.w[:, a:b], "dw%d" % k)
 
     lane = iota(new("aI", 1), [[0, 1]], 0, 1)
-    jj = iota(new("aF", 16), [[1, 16]])
+    jj = iota(new("aF", 64), [[0, 4], [1, 16]])
     bb = iota(new("aF", 32), [[1, 32]])
     t_y = iota(new("aF", 6), [[1, 3], [0, 2]], 16 * r)
     t_tr = iota(new("aF", 16), [[-1, 16]], 79)
     t_d = iota(new("aF", 8), [[16, 4], [0, 2]])
     t_g = iota(new("aF", 8), [[32, 4], [0, 2]])
+    np1 = iota(new("aF", 256), [[-128, 8], [0, 2], [-1, 16]], -(8 * r + 2))
+    np2 = iota(new("aF", 256), [[0, 16], [-56, 2], [0, 8]])
     ones = const(new("aH", 128), 1)
     X, M = new("aH", 130), new("aH", 129)
     const(sub(X, 0, 1), 0)
@@ -208,29 +210,25 @@ def rank_program(g, core, T, topo):
     const(sub(M, 0, 1), 1000)
     const(sub(M, 128, 129), 1000)
     F1 = lambda: new("aF", 1)
+    fill(V("ut", 8, 512), 0.0)
     zero = fill(new("aU", 8), 0)
     bF = cp(F1(), ts(new("aI", 1), lane, 31, A.bitwise_and))
-    lo = ts(F1(), bF, 16.0, LT)
-    hi = ts(F1(), bF, 16.0, GE)
-    j = tt(F1(), tt(F1(), ts(F1(), bF, -2.0, MUL, 31.0, ADD), hi, MUL), bF, ADD)
-    c0 = tt(F1(), ts(F1(), j, 15.0, EQ, 0.0625, MUL), ts(F1(), j, 0.0, NE, 0.0625, MUL), ADD)
-    c1 = ts(F1(), ts(F1(), j, 0.0, EQ, -8.0, MUL), 16.0, ADD)
-    d = ts(new("aF", 16), jj, j, SUB)
-    f1 = ts(new("aF", 16), d, 0.0, EQ, c0, MUL)
-    f2 = ts(new("aF", 16), d, 1.0, EQ, c1, MUL)
-    f3 = ts(new("aF", 16), d, 2.0, EQ, 1024.0, MUL)
-    f4 = ts(new("aF", 16), d, 3.0, GE)
-    f12 = tt(new("aF", 16), f1, f2, ADD)
-    f34 = tt(new("aF", 16), f3, f4, ADD)
-    ft = new("aF", 256)
-    tt(sub(ft, 0, 16), f12, f34, ADD)
-    for n in (16, 32, 64, 128):
-        cp(sub(ft, n, 2 * n), sub(ft, 0, n))
-    n1 = ts(F1(), j, 0.0, EQ, 2.0 / 1024, MUL)
-    n2 = ts(F1(), j, 13.5, LT, 2.0 / 1024, MUL)
-    n3 = ts(F1(), j, 14.0, EQ, 2.0, MUL)
-    n4 = ts(F1(), j, 15.0, EQ, 32.0, MUL)
-    nrm = tt(F1(), tt(F1(), n1, n2, ADD), tt(F1(), n3, n4, ADD), ADD)
+    w = act(F1(), bF, AF.Abs, bias=-15.5)
+    first = act(F1(), w, AF.Relu, bias=-14.5)
+    last = act(F1(), w, AF.Relu, -1.0, 1.5)
+    last2 = act(F1(), w, AF.Relu, -1.0, 2.5)
+    c0 = act(F1(), last, AF.Identity, 0.0625, act(F1(), first, AF.Identity, -0.0625, 0.0625))
+    c1 = act(F1(), first, AF.Identity, -8.0, 16.0)
+    e = 2.0 / 1024
+    nrm = act(F1(), first, AF.Identity, e, act(F1(), last, AF.Identity, 28.0 + e, act(F1(), last2, AF.Identity, 2.0 - e, e)))
+    d = ts(new("aF", 64), jj, w, ADD, -15.5, ADD)
+    f3 = ts(new("aF", 64), d, 2.0, EQ, 1024.0, MUL)
+    f4 = ts(new("aF", 64), d, 3.0, GE)
+    f34 = tt(new("aF", 64), f3, f4, ADD)
+    f1 = ts(new("aF", 64), d, 0.0, EQ, c0, MUL)
+    f2 = ts(new("aF", 64), d, 1.0, EQ, c1, MUL)
+    f12 = tt(new("aF", 64), f1, f2, ADD)
+    ft = tt(new("aF", 64), f12, f34, ADD)
 
     quant(V("uq", 0, 128), V("us", 0, 128), V("ut", 0, 512))
     pickc(V("rq", 0, 128), V("uq", 0, 128), zero)
@@ -242,7 +240,9 @@ def rank_program(g, core, T, topo):
            V("xq", 128 * h, 128 * h + 128), V("xs", 128 * h, 128 * h + 128), True, True)
     for h in (0, 1):
         ts(sub(sgn, 128 * h, 128 * h + 128), V("ps", 512 * h, 512 * h + 128), 0.0, A.is_gt, -0.5, ADD)
-    cells = scan(new("aF", 256), ft, sgn)
+    cells = new("aF", 256)
+    for a in (0, 64, 128, 192):
+        scan(sub(cells, a, a + 64), ft, sub(sgn, a, a + 64))
     own = V("sg", 16 * r, 16 * r + 16)
     ts(own, sub(cells, 15, 256, 16), nrm, MUL)
     send([(k, own, own) for k in others], False, "rsign", "lsign", [own])
@@ -262,11 +262,10 @@ def rank_program(g, core, T, topo):
     t_st = iota(new("aF", 128), [[64, 8], [0, 16]], Z0)
     st0 = asel(new("aF", 128), t_st, [[0, 8], [1, 16]], EQ, 0.0, 0)
     r16 = asel(new("aF", 256), onef, [[0, 16], [1, 16]], NE, 0.0, 0)
-    np1 = iota(new("aF", 256), [[-128, 8], [0, 2], [-1, 16]], -(8 * r + 2))
-    np2 = iota(new("aF", 256), [[0, 16], [-56, 2], [0, 8]])
 
+    lo = ts(F1(), bF, 16.0, LT)
+    hi = ts(F1(), bF, 16.0, GE)
     d0 = act(new("aH", 128), ones, AF.Copy, scale=lo)
-    m0 = act(F1(), lo, AF.Copy, scale=-1.0)
     m1 = act(F1(), hi, AF.Copy, scale=-1.0)
     m2 = act(F1(), hi, AF.Copy, scale=-1024.0)
     one0 = ts(F1(), bF, 0.0, EQ)
@@ -285,7 +284,17 @@ def rank_program(g, core, T, topo):
     quant(V("zq", 0, 128), V("zs", 0, 128), V("zt", 0, 512))
     dma("y", V("laq", 0, Z0), V("zq", 0, Z0), "dz0", True)
     dma("y", V("las", 0, Z0), V("zs", 0, Z0), "dz1")
-    quant(V("wq", 0, 512), V("ws", 0, 512), V("wt", 0, 2048))
+    for a, b in ((0, 512), (512, 1024)):
+        quant(V("wq", a, b), V("ws", a, b), V("wt", 4 * a, 4 * b))
+    off_t = ts(new("aU", 8), t_g, 15.0, ADD)
+    off_g = ts(new("aU", 8), t_g, iF, ADD)
+    low8 = ts(F1(), iF, 7.5, A.is_gt, 56.0, MUL)
+    ln = ts(F1(), tt(F1(), low8, iF, ADD), 1.5, ADD)
+    npt = tt(new("aF", 256), np1, np2, ADD)
+    hl = ts(F1(), iF, 14.5, LT, 1024.0, MUL)
+    hr = ts(F1(), iF, 0.5, A.is_gt, float(1 << 20), MUL)
+    m0 = tt(F1(), ts(F1(), hl, -1.0, MUL, -1.0, ADD), lo, MUL)
+    m3 = tt(F1(), tt(F1(), hr, hl, SUB), lo, MUL)
 
     ab = act(new("aH", 128), V("sg", 0, 128), AF.Abs)
     tt(sub(M, 1, 128), V("sg", 0, 127), V("sg", 1, 128), MUL)
@@ -295,7 +304,10 @@ def rank_program(g, core, T, topo):
     scan(sub(X, 1, 129), d0, av, one0)
 
     Y = gather(new("aH", 96), X, off_y)
+    ZR = tr(new("aH", 128), sub(X, 1, 129))
     YT = tr(new("aH", 96), Y)
+    SR = scan(new("aF", 128), rs, ZR)
+    TG = gather(new("aF", 128), SR, off_t, "s")
     S6 = scan(new("aF", 96), sub(rs, 0, 96), YT)
     V6 = tt(new("aI", 96), S6, YT, MUL)
     A6 = ts(new("aI", 96), V6, 56 | 1 << 20, A.bitwise_and)
@@ -343,26 +355,17 @@ def rank_program(g, core, T, topo):
         for n, m in (("laq", "rlc"), ("las", "rls")):
             note(V(n, Z0 + 64 * k, Z0 + 64 * k + NC), True, None, m, count[m], {})
 
-    off_t = ts(new("aU", 8), t_g, 15.0, ADD)
-    ZR = tr(new("aH", 128), sub(X, 1, 129))
-    SR = scan(new("aF", 128), rs, ZR)
-    TG = gather(new("aF", 128), SR, off_t, "s")
-    low8 = ts(F1(), iF, 7.5, A.is_gt, 56.0, MUL)
-    VR = tt(new("aI", 128), SR, ZR, MUL)
-    ln = ts(F1(), tt(F1(), low8, iF, ADD), 1.5, ADD)
     nb = act(new("aF", 8), t_nb, AF.Identity, bias=ln)
+    VR = tt(new("aI", 128), SR, ZR, MUL)
     AR = ts(new("aI", 128), VR, 56 | 1 << 20, A.bitwise_and)
     TF = tr(new("aF", 128), TG)
     acc = new("aF", 8)
     for c in range(8):
         act(new("aH", 128), TF, AF.Sign, -1.0, sub(nb, c, c + 1), sub(acc, c, c + 1))
     ts(sub(E, 0, 128), AR, float((1 << 20) + 56 - 8 * r), EQ)
-    off_g = ts(new("aU", 8), t_g, iF, ADD)
-    hl = ts(F1(), iF, 14.5, LT, 1024.0, MUL)
     H1 = tt(new("aH", 127), sub(E, 0, 127), sub(E, 2, 129), MAX)
     w1 = tt(new("aF", 128), VR, sub(E, 0, 128), MUL)
     H2 = tt(new("aH", 127), H1, sub(E, 1, 128), MAX)
-    hr = ts(F1(), iF, 0.5, A.is_gt, 2048.0, MUL)
     w2 = new("aF", 128)
     tt(sub(w2, 1, 128), sub(w1, 1, 128), H2, SUB)
     wd = gather(new("aF", 128), sub(w2, 16, 128), off_g)
@@ -381,13 +384,12 @@ def rank_program(g, core, T, topo):
     xn = scan(new("aF", 128), dn, h3)
     zn = tr(new("aF", 128), xn)
     sn = scan(new("aF", 128), rs, zn)
-    m3 = tt(F1(), tt(F1(), hl, hr, ADD), lo, MUL)
     pd = gather(new("aF", 128), sub(sn, 16, 128), off_g)
     tr(sub(pc, 1, 129), pd)
     p1 = act(new("aF", 128), sub(pc, 1, 129), AF.Identity, m0, m3)
     p2 = act(new("aF", 128), sub(pc, 0, 128), AF.Copy, m1)
     p3 = ts(new("aF", 128), sub(pc, 2, 130), m2, MUL)
-    npt = tt(new("aF", 256), np1, np2, ADD)
+    quant(V("wq", 1024, 1280), V("ws", 1024, 1280), V("wt", 4096, 5120))
     p4 = tt(new("aF", 128), p1, p3, ADD)
     tt(sub(pt, 0, 128), p4, p2, ADD)
     gp = gather(new("aF", 256), pt, rp, "s")
@@ -397,21 +399,18 @@ def rank_program(g, core, T, topo):
     op = tt(new("aF", 256), oh, gp, MUL)
     ot = tr(new("aF", 256), op)
     os_ = scan(new("aF", 256), r16, ot)
-    ai = cp(new("aI", 8), sub(os_, 15, 256, 32))
-    bi = cp(new("aI", 8), sub(os_, 31, 256, 32))
-    li = new("aI", 40)
-    k0 = ts(sub(li, 0, 8), ai, 1023, A.bitwise_and)
-    ts(sub(li, 8, 16), bi, 1023, A.bitwise_and)
-    ts(sub(li, 16, 24), bi, 10, A.arith_shift_right)
-    fl = ts(new("aI", 8), ai, 10, A.arith_shift_right, 1, A.bitwise_and)
-    fr = ts(new("aI", 8), ai, 11, A.arith_shift_right)
-    kl = ts(new("aI", 8), k0, -1.0, ADD)
+    ab2 = cp(new("aI", 16), sub(os_, 15, 256, 16))
+    va, vb = sub(ab2, 0, 16, 2), sub(ab2, 1, 16, 2)
+    li, lu = new("aI", 40), new("aU", 40)
+    k0 = ts(sub(li, 0, 8), va, 1023, A.bitwise_and)
+    ts(sub(li, 8, 16), vb, 1023, A.bitwise_and)
+    ts(sub(li, 16, 24), vb, 10, A.arith_shift_right)
+    ts(sub(li, 24, 32), va, 10, A.arith_shift_right, 1023, A.bitwise_and)
+    fr = ts(new("aI", 8), va, 20, A.arith_shift_right)
     kr = ts(new("aI", 8), k0, 1.0, ADD)
-    tt(sub(li, 24, 32), kl, fl, MUL)
+    cp(sub(lu, 0, 32), sub(li, 0, 32))
     tt(sub(li, 32, 40), kr, fr, MUL)
-    lu = cp(new("aU", 40), li)
-    for a, b in ((512, 1024), (1024, 1280)):
-        quant(V("wq", a, b), V("ws", a, b), V("wt", 4 * a, 4 * b))
+    cp(sub(lu, 32, 40), sub(li, 32, 40))
 
     tk = lambda n, k: V(n, 128 * k, 128 * k + 128)
     lk = lambda k: sub(lu, 8 * k, 8 * k + 8)

@@ -310,8 +310,11 @@ def rank_program(g, core, T, topo):
     TG = gather(new("aF", 128), SR, off_t, "s")
     S6 = scan(new("aF", 96), sub(rs, 0, 96), YT)
     V6 = tt(new("aI", 96), S6, YT, MUL)
+    VR = tt(new("aI", 128), SR, ZR, MUL)
     A6 = ts(new("aI", 96), V6, 56 | 1 << 20, A.bitwise_and)
+    AR = ts(new("aI", 128), VR, 56 | 1 << 20, A.bitwise_and)
     E6 = ts(new("aH", 96), A6, ge, EQ)
+    ts(sub(E, 0, 128), AR, float((1 << 20) + 56 - 8 * r), EQ)
     a1 = tt(new("aH", 16), sub(E6, 16, 32), sub(E6, 80, 96), MAX)
     a2 = tt(new("aH", 16), sub(E6, 47, 63), sub(E6, 49, 65), MAX)
     a3 = tt(new("aH", 16), a1, sub(E6, 48, 64), MAX)
@@ -327,16 +330,16 @@ def rank_program(g, core, T, topo):
     off = ts(new("aU", 16), q3, base, ADD)
     run("v", [win], [off, val], lambda e: e.tensor_copy(ap(win).indirect(ap(off)), ap(val)))
     D = gather(new("aH", 128), sub(win, 0, 64), off_d)
-    DT = tr(new("aH", 128), D)
+    DT = new("aH", 256)
+    tr(sub(DT, 0, 128), D)
+    tr(sub(DT, 128, 256), D)
     lc = new("aH", 32)
     for a in range(4):
-        for h in (0, 1):
-            o = sub(lc, 8 * a + 4 * h, 8 * a + 4 * h + 4, 1, 0, 32)
-            i = sub(DT, 16 * h, 128, 32, 32 * a, 32 * a + 32)
-            if a % 2:
-                run("s", [o], [i], lambda e: e.activation(ap(o), ap(i), AF.Copy))
-            else:
-                cp(o, i)
+        o, i = sub(lc, 8 * a, 8 * a + 8, 1, 0, 32), sub(DT, 0, 256, 36, 32 * a, 32 * a + 32)
+        if a % 2:
+            run("s", [o], [i], lambda e: e.activation(ap(o), ap(i), AF.Copy))
+        else:
+            cp(o, i)
     cp(sub(lc, 0, 32, 1, 32, 64), sub(lc, 0, 32, 1, 0, 32))
     lw = new("aU", 32)
     cp(sub(lw, 0, 32, 1, 0, 64), sub(lc, 0, 32, 1, 0, 64))
@@ -356,13 +359,10 @@ def rank_program(g, core, T, topo):
             note(V(n, Z0 + 64 * k, Z0 + 64 * k + NC), True, None, m, count[m], {})
 
     nb = act(new("aF", 8), t_nb, AF.Identity, bias=ln)
-    VR = tt(new("aI", 128), SR, ZR, MUL)
-    AR = ts(new("aI", 128), VR, 56 | 1 << 20, A.bitwise_and)
     TF = tr(new("aF", 128), TG)
     acc = new("aF", 8)
     for c in range(8):
         act(new("aH", 128), TF, AF.Sign, -1.0, sub(nb, c, c + 1), sub(acc, c, c + 1))
-    ts(sub(E, 0, 128), AR, float((1 << 20) + 56 - 8 * r), EQ)
     H1 = tt(new("aH", 127), sub(E, 0, 127), sub(E, 2, 129), MAX)
     w1 = tt(new("aF", 128), VR, sub(E, 0, 128), MUL)
     H2 = tt(new("aH", 127), H1, sub(E, 1, 128), MAX)
@@ -416,12 +416,12 @@ def rank_program(g, core, T, topo):
     lk = lambda k: sub(lu, 8 * k, 8 * k + 8)
     for k in range(5):
         pickc(tk("tq", k), V("laq", 0, LW), lk(k))
-    for k in (0, 3, 1, 4, 2):
-        gather(tk("ts", k), V("las", 0, LW), lk(k), "v" if k > 2 else "s")
-    for k in (0, 3, 1, 4, 2):
+    for k in range(5):
+        gather(tk("ts", k), V("las", 0, LW), lk(k), "v" if k > 3 else "s")
+    for k in range(5):
         for o in (0, 1):
             a = 128 * (2 * k + o)
-            mm(V("ps", 1024 + 512 * o, 1152 + 512 * o), V("wq", a, a + 128), V("ws", a, a + 128), tk("tq", k), tk("ts", k), k == 0, k == 2)
+            mm(V("ps", 1024 + 512 * o, 1152 + 512 * o), V("wq", a, a + 128), V("ws", a, a + 128), tk("tq", k), tk("ts", k), k == 0, k == 4)
     cp(V("yo", 0, 128), V("ps", 1024, 1152))
     act(V("yo", 128, 256), V("ps", 1536, 1664), AF.Copy)
     dma("y", T.y[:, 0:128], V("yo", 0, 128), "dy0")

@@ -2,19 +2,23 @@ from concourse.bass import DstId, RemoteDMATransfer
 from concourse.mybir import dt, AluOpType, ActivationFunctionType, AxisListType
 
 N = 8
-NC = 56
-Z0 = 16
-LW = Z0 + 64 * N
+NS = 16
+NC = 5 * NS
+SL = NC + 16
+LW = SL * N + 16 + 128
+PW = 16 + 256 + 16 + 128
+MID = 144
+KW = (1, 3, 0, 4, 2)
 F8, U8, BF, F32 = "float8_e4m3fn_x4", "uint8", "bfloat16", "float32"
-SCRATCH = {"aF": ("sbuf", [128, 10240], F32), "aH": ("sbuf", [128, 5120], BF), "aI": ("sbuf", [128, 768], "int32"),
-           "aU": ("sbuf", [128, 512], "uint16"), "sg": ("sbuf", [128, 128], BF), "xt": ("sbuf", [128, 1024], BF),
-           "ut": ("sbuf", [128, 512], BF), "wt": ("sbuf", [128, 5120], BF), "zt": ("sbuf", [128, 512], BF),
+SCRATCH = {"aF": ("sbuf", [128, 4096], F32), "aH": ("sbuf", [128, 6144], BF), "aI": ("sbuf", [128, 256], "int32"),
+           "aU": ("sbuf", [128, 512], "uint16"), "sg": ("sbuf", [128, 128], BF), "xt": ("sbuf", [128, 1088], BF),
+           "uc": ("sbuf", [128, 16], BF), "ut": ("sbuf", [128, 512], BF), "wt": ("sbuf", [128, 5120], BF), "zt": ("sbuf", [128, 512], BF),
            "yo": ("sbuf", [128, 256], F32), "ps": ("psum", [128, 2048], F32)}
-for _n, _w in (("x", 256), ("u", 128), ("r", 128), ("w", 1280), ("z", 128), ("sl", 512), ("la", LW), ("t", 640)):
+for _n, _w in (("x", 256), ("u", 128), ("w", 1280), ("gr", PW), ("sl", NC * 7), ("la", LW), ("t", 640)):
     SCRATCH[_n + "q"] = ("sbuf", [128, _w], F8)
     SCRATCH[_n + "s"] = ("sbuf", [128, _w], U8)
-DMAS = ["dx0", "dx1", "du", "dw0", "dw1", "dw2", "dz0", "dz1", "dy0", "dy1"]
-SEMAPHORES = ["qv", "qs", "qt", "qg"] + DMAS + ["rsign", "lsign", "rlc", "rls", "lland"]
+DMAS = ["dx0", "dx1", "du", "dw0", "dw1", "dw2", "dy0", "dy1"]
+SEMAPHORES = ["qv", "qs", "qt", "qg"] + DMAS + ["rsign", "lsign", "rhc", "rhs", "lhalo", "rlc", "rls", "lland"]
 A = AluOpType
 AF = ActivationFunctionType
 AX = AxisListType.X
@@ -34,21 +38,19 @@ def rank_program(g, core, T, topo):
     used = {"aF": 0, "aH": 0, "aI": 0, "aU": 0}
     unit = {"aF": 8, "aH": 16, "aI": 8, "aU": 16}
 
-    def V(name, a, b, p=0, e=128, step=1):
-        return (name, a, b, p, e, step)
+    def V(name, a, b, step=1):
+        return (name, a, b, step)
 
     def new(arena, n):
         a = used[arena]
         used[arena] = a + -(-n // unit[arena]) * unit[arena]
         return V(arena, a, a + n)
 
-    def sub(v, a, b, step=1, p=0, e=128):
-        return V(v[0], v[1] + a, v[1] + b, p, e, step)
+    def sub(v, a, b, step=1):
+        return V(v[0], v[1] + a, v[1] + b, step)
 
     def ap(v):
-        if v[3] == 0 and v[4] == 128:
-            return T[v[0]][:, v[1]:v[2]:v[5]] if v[5] != 1 else T[v[0]][:, v[1]:v[2]]
-        return T[v[0]][v[3]:v[4], v[1]:v[2]:v[5]] if v[5] != 1 else T[v[0]][v[3]:v[4], v[1]:v[2]]
+        return T[v[0]][:, v[1]:v[2]:v[3]] if v[3] != 1 else T[v[0]][:, v[1]:v[2]]
 
     def note(v, write, q, sem, val, clock):
         hist.setdefault(v[0], []).append((v, write, q, sem, val, clock))
@@ -58,9 +60,11 @@ def rank_program(g, core, T, topo):
         for group, out in ((outs, True), (ins, False)):
             for v in group:
                 for (o, write, oq, sem, val, clock) in hist.get(v[0], []):
-                    if not (write or out) or o[1] >= v[2] or v[1] >= o[2] or o[3] >= v[4] or v[3] >= o[4]:
+                    if not (write or out) or o[1] >= v[2] or v[1] >= o[2]:
                         continue
                     if not write and oq == q and sem == csem.get(q):
+                        continue
+                    if v[3] == o[3] and v[3] > 1 and (v[1] - o[1]) % v[3]:
                         continue
                     if val > need.get(sem, (0, None))[0]:
                         need[sem] = (val, clock)
@@ -132,14 +136,10 @@ def rank_program(g, core, T, topo):
             run("s", [o], [win, off], lambda e: e.activation(ap(o), ap(win).indirect(ap(off)), AF.Copy))
         return o
 
-    def act(o, i, func, scale=1.0, bias=0.0, accum=None):
-        ins, outs = [i], [o]
+    def act(o, i, func, scale=1.0, bias=0.0):
+        ins = [i]
         a, b = sc(scale, ins), sc(bias, ins)
-        if accum is not None:
-            outs.append(accum)
-            run("s", outs, ins, lambda e: e.activation(ap(o), ap(i), func, bias=b, scale=a, accum_out=ap(accum)))
-        else:
-            run("s", outs, ins, lambda e: e.activation(ap(o), ap(i), func, bias=b, scale=a))
+        run("s", [o], ins, lambda e: e.activation(ap(o), ap(i), func, bias=b, scale=a))
         return o
 
     def iota(o, pattern, base=0, lane=0):
@@ -153,14 +153,12 @@ def rank_program(g, core, T, topo):
         run("g", [o], [i], lambda e: e.affine_select(ap(o), ap(i), pattern, op, c, base, 0))
         return o
 
-    def dma(q, o, i, sem, bits=False):
-        def call(e):
-            a = ap(o) if isinstance(o, tuple) else o
-            b = ap(i) if isinstance(i, tuple) else i
-            return e.dma_start(a.bitcast(dt.uint8), b.bitcast(dt.uint8)) if bits else e.dma_start(a, b)
-        run(q, [v for v in (o,) if isinstance(v, tuple)], [v for v in (i,) if isinstance(v, tuple)], call, sem, 16)
+    def dma(q, o, i, sem):
+        run(q, [v for v in (o,) if isinstance(v, tuple)], [v for v in (i,) if isinstance(v, tuple)],
+            lambda e: e.dma_start(ap(o) if isinstance(o, tuple) else o, ap(i) if isinstance(i, tuple) else i), sem, 16)
 
-    def quant(q, s, i):
+    def quant(n, a, b, t, c):
+        q, s, i = V(n + "q", a, b), V(n + "s", a, b), V(t, c, c + 4 * (b - a))
         run("v", [q, s], [i], lambda e: e.quantize_mx(ap(q), ap(s), ap(i)))
 
     def pickc(cq, wq, off):
@@ -173,7 +171,7 @@ def rank_program(g, core, T, topo):
 
     others = [d for d in range(N) if d != r]
 
-    def send(pairs, bits, rsem, lsem, ins):
+    def send(pairs, width, bits, rsem, lsem, ins, senders):
         sync("g", [], ins)
         xs = []
         for k, (d, src, dst) in enumerate(pairs):
@@ -182,36 +180,33 @@ def rank_program(g, core, T, topo):
             a, b = ap(src), ap(dst)
             if bits:
                 a, b = a.bitcast(dt.uint8), b.bitcast(dt.uint8)
-            xs.append(RemoteDMATransfer(dst_ids=[DstId(rid=rid, pnc=pid)], dma_engine_mask=1 << topo.engines(core, to)[k],
+            mask = sum(1 << e for e in topo.engines(core, to)[width * k:width * k + width])
+            xs.append(RemoteDMATransfer(dst_ids=[DstId(rid=rid, pnc=pid)], dma_engine_mask=mask,
                                         remote_sem=T.sem[rsem], src=a, dst=b))
         g.remote_dma_fused(xs, local_sem=T.sem[lsem])
-        count[lsem] = count.get(lsem, 0) + len(xs)
-        count[rsem] = count.get(rsem, 0) + len(xs)
+        count[lsem] = count.get(lsem, 0) + width * len(xs)
+        count[rsem] = count.get(rsem, 0) + width * senders
 
-    dma("s", V("ut", 0, 8), T.u[:, 0:8], "du")
-    dma("y", V("xt", 0, 512), T.x[:, 0:512], "dx0")
-    dma("s", V("xt", 512, 1024), T.x[:, 512:1024], "dx1")
+    F1 = lambda: new("aF", 1)
+    dma("s", V("uc", 0, 8), T.u[:, 0:8], "du")
+    dma("y", V("xt", 64, 576), T.x[:, 0:512], "dx0")
+    dma("s", V("xt", 576, 1088), T.x[:, 512:1024], "dx1")
     for k, (a, b) in enumerate(((0, 2048), (2048, 4096), (4096, 5120))):
         dma("y", V("wt", a, b), T.w[:, a:b], "dw%d" % k)
 
     lane = iota(new("aI", 1), [[0, 1]], 0, 1)
     jj = iota(new("aF", 64), [[0, 4], [1, 16]])
-    bb = iota(new("aF", 32), [[1, 32]])
-    t_y = iota(new("aF", 6), [[1, 3], [0, 2]], 16 * r)
-    t_tr = iota(new("aF", 16), [[-1, 16]], 79)
-    t_d = iota(new("aF", 8), [[16, 4], [0, 2]])
-    t_g = iota(new("aF", 8), [[32, 4], [0, 2]])
-    np1 = iota(new("aF", 256), [[-128, 8], [0, 2], [-1, 16]], -(8 * r + 2))
-    np2 = iota(new("aF", 256), [[0, 16], [-56, 2], [0, 8]])
-    ones = const(new("aH", 128), 1)
-    X, M = new("aH", 130), new("aH", 129)
-    const(sub(X, 0, 1), 0)
-    const(sub(X, 129, 130), 0)
-    const(sub(M, 0, 1), 1000)
-    const(sub(M, 128, 129), 1000)
-    F1 = lambda: new("aF", 1)
-    fill(V("ut", 8, 512), 0.0)
-    zero = fill(new("aU", 8), 0)
+    t_y = const(new("aF", 2), 16 * r)
+    t_d = new("aF", 16)
+    iota(sub(t_d, 0, 2), [[0, 2]], 383 - 8 * r)
+    if r > 0:
+        iota(sub(t_d, 2, 2 + 2 * r), [[-8, r], [0, 2]], 383)
+    if r < N - 1:
+        iota(sub(t_d, 2 + 2 * r, 16), [[-8, N - 1 - r], [0, 2]], 383 - 8 * (r + 1))
+    t_l = iota(new("aF", 3), [[16, 3]], -1)
+    t_tr = iota(new("aF", 16), [[1, 16]], (1 << 20) - 256)
+    np1 = iota(new("aF", 256), [[128, 8], [0, 4], [1, 8]], 8 * r + 1)
+    ones = fill(new("aH", 128), 1.0)
     bF = cp(F1(), ts(new("aI", 1), lane, 31, A.bitwise_and))
     w = act(F1(), bF, AF.Abs, bias=-15.5)
     first = act(F1(), w, AF.Relu, bias=-14.5)
@@ -219,208 +214,150 @@ def rank_program(g, core, T, topo):
     last2 = act(F1(), w, AF.Relu, -1.0, 2.5)
     c0 = act(F1(), last, AF.Identity, 0.0625, act(F1(), first, AF.Identity, -0.0625, 0.0625))
     c1 = act(F1(), first, AF.Identity, -8.0, 16.0)
-    e = 2.0 / 1024
-    nrm = act(F1(), first, AF.Identity, e, act(F1(), last, AF.Identity, 28.0 + e, act(F1(), last2, AF.Identity, 2.0 - e, e)))
     d = ts(new("aF", 64), jj, w, ADD, -15.5, ADD)
     f3 = ts(new("aF", 64), d, 2.0, EQ, 1024.0, MUL)
     f4 = ts(new("aF", 64), d, 3.0, GE)
-    f34 = tt(new("aF", 64), f3, f4, ADD)
     f1 = ts(new("aF", 64), d, 0.0, EQ, c0, MUL)
     f2 = ts(new("aF", 64), d, 1.0, EQ, c1, MUL)
+    f34 = tt(new("aF", 64), f3, f4, ADD)
     f12 = tt(new("aF", 64), f1, f2, ADD)
-    ft = tt(new("aF", 64), f12, f34, ADD)
+    ft = new("aH", 256)
+    tt(sub(ft, 0, 64), f12, f34, ADD)
 
-    quant(V("uq", 0, 128), V("us", 0, 128), V("ut", 0, 512))
-    pickc(V("rq", 0, 128), V("uq", 0, 128), zero)
-    gather(V("rs", 0, 128), V("us", 0, 128), zero, "s")
-    sgn = new("aF", 256)
+    for t in (0, 1):
+        ts(V("ut", t, 512, 4), ones, V("uc", t, t + 1), MUL)
+    for t in (2, 3):
+        act(V("ut", t, 512, 4), ones, AF.Identity, 0.0, V("uc", t, t + 1))
+    for a in (64, 128, 192):
+        act(sub(ft, a, a + 64), sub(ft, 0, 64), AF.Copy)
+    e = 2.0 / 1024
+    nrm = act(F1(), first, AF.Identity, e, act(F1(), last, AF.Identity, 28.0 + e, act(F1(), last2, AF.Identity, 2.0 - e, e)))
+    quant("u", 0, 128, "ut", 0)
+    sgn, cells = new("aH", 256), new("aH", 256)
     for h in (0, 1):
-        quant(V("xq", 128 * h, 128 * h + 128), V("xs", 128 * h, 128 * h + 128), V("xt", 512 * h, 512 * h + 512))
-        mm(V("ps", 512 * h, 512 * h + 128), V("rq", 0, 128), V("rs", 0, 128),
+        quant("x", 128 * h, 128 * h + 128, "xt", 64 + 512 * h)
+        mm(V("ps", 512 * h, 512 * h + 128), V("uq", 0, 128), V("us", 0, 128),
            V("xq", 128 * h, 128 * h + 128), V("xs", 128 * h, 128 * h + 128), True, True)
+    halo = [(k, a, b) for k, a, b in ((r + 1, 240, 0), (r - 1, 0, 272)) if 0 <= k < N]
+
+    def edges(n, bits, rsem):
+        at = lambda m, a: V(m + n, a, a + 16)
+        send([(k, at("x", a), at("gr", b)) for k, a, b in halo], 4, bits, rsem, "lhalo", [at("x", a) for k, a, b in halo], len(halo))
+        for k, a, b in halo:
+            note(at("gr", 0 if k < r else 272), True, None, rsem, count[rsem], {})
+
+    edges("q", True, "rhc")
     for h in (0, 1):
         ts(sub(sgn, 128 * h, 128 * h + 128), V("ps", 512 * h, 512 * h + 128), 0.0, A.is_gt, -0.5, ADD)
-    cells = new("aF", 256)
-    for a in (0, 64, 128, 192):
-        scan(sub(cells, a, a + 64), ft, sub(sgn, a, a + 64))
+    scan(cells, ft, sgn)
     own = V("sg", 16 * r, 16 * r + 16)
     ts(own, sub(cells, 15, 256, 16), nrm, MUL)
-    send([(k, own, own) for k in others], False, "rsign", "lsign", [own])
+    send([(k, own, own) for k in others], 1, False, "rsign", "lsign", [own], N - 1)
     for k in others:
         note(V("sg", 16 * k, 16 * k + 16), True, None, "rsign", count["rsign"], {})
+    edges("s", False, "rhs")
 
-    onef = const(new("aF", 256), 1)
-    rs0 = asel(new("aF", 128), sub(onef, 0, 128), [[0, 4], [1, 32]], NE, 0.0, 0)
-    rs = asel(new("aF", 128), rs0, [[0, 4], [1, 32]], NE, -1.0, -16)
-    win = new("aH", 384)
-    const(sub(win, 0, 64), 0)
-    val = iota(new("aH", 256), [[-1, 16], [16, 16]], 15)
-    tv, pt, pc, ec, E = new("aF", 129), new("aF", 129), new("aF", 130), new("aH", 130), new("aH", 129)
-    for v, a in ((E, 128), (ec, 0), (ec, 129), (tv, 128), (pc, 0), (pc, 129), (pt, 128)):
-        const(sub(v, a, a + 1), 0)
-    t_nb = iota(new("aF", 8), [[128, 8]], 8 * r)
-    t_st = iota(new("aF", 128), [[64, 8], [0, 16]], Z0)
-    st0 = asel(new("aF", 128), t_st, [[0, 8], [1, 16]], EQ, 0.0, 0)
-    r16 = asel(new("aF", 256), onef, [[0, 16], [1, 16]], NE, 0.0, 0)
+    base = iota(new("aH", 256), [[-1, 16], [16, 16]], 31 - MID)
+    win = const(new("aH", 384), MID)
+    onef = const(new("aF", 32), 1)
+    rs = asel(new("aF", 32), asel(new("aF", 32), onef, [[1, 32]], NE, 0.0, 0), [[1, 32]], NE, -1.0, -16)
+    np2 = iota(new("aF", 256), [[0, 16], [64, 2], [0, 8]])
+    r32 = asel(new("aH", 256), const(new("aH", 256), 1), [[0, 8], [1, 32]], NE, 0.0, 0)
 
     lo = ts(F1(), bF, 16.0, LT)
-    hi = ts(F1(), bF, 16.0, GE)
-    d0 = act(new("aH", 128), ones, AF.Copy, scale=lo)
-    m1 = act(F1(), hi, AF.Copy, scale=-1.0)
-    m2 = act(F1(), hi, AF.Copy, scale=-1024.0)
     one0 = ts(F1(), bF, 0.0, EQ)
     iF = cp(F1(), ts(new("aI", 1), lane, 15, A.bitwise_and))
-    gF = cp(F1(), ts(new("aI", 1), lane, 4, A.arith_shift_right))
-    off_y = ts(new("aU", 6), t_y, iF, ADD)
-    off_d = ts(new("aU", 8), t_d, iF, ADD)
-    i16 = ts(F1(), iF, 16.0, MUL)
-    ge = ts(F1(), gF, -8.0, MUL, float((1 << 20) + 56), ADD)
+    high = ts(F1(), iF, 8.0, GE, -56.0, MUL)
+    e1, n1 = ts(F1(), bF, 1.0, EQ), ts(F1(), bF, 1.0, NE)
+    e3, n3 = ts(F1(), bF, 3.0, EQ), ts(F1(), bF, 3.0, NE)
+    off_y = ts(new("aU", 2), t_y, iF, ADD)
+    sl8 = tt(F1(), high, iF, SUB)
+    la = ts(new("aF", 3), t_l, iF, ADD, 0.0, MAX)
+    lb = ts(new("aI", 3), la, 0.2, MUL, -0.4, ADD)
+    off_d = ts(new("aU", 16), t_d, sl8, ADD)
+    lc = ts(new("aF", 3), lb, 27.0, MUL)
+    ld = tt(new("aF", 3), lc, la, ADD)
+    off_l = ts(new("aU", 3), ld, 255.0, MIN)
+    d0 = act(new("aH", 128), ones, AF.Copy, scale=lo)
+    i16 = act(F1(), iF, AF.Copy, scale=16.0)
     trash = act(new("aF", 16), t_tr, AF.Identity, bias=i16)
-    top = ts(F1(), hi, 16.0, MUL, 16.0, ADD)
-    mk1 = ts(new("aF", 32), bb, bF, GE)
-    mk2 = ts(new("aF", 32), bb, top, LT)
-    mk = tt(new("aF", 32), mk1, mk2, MUL)
+    sx = act(F1(), bF, AF.Identity, bias=-2.0)
+    sx2 = act(F1(), sx, AF.Square)
+    delta = act(F1(), act(F1(), sx2, AF.Identity, 7.0 / 3, -4.0 / 3), AF.Copy, scale=sx)
+    z1 = act(F1(), e1, AF.Identity, float(MID + 1), delta)
+    z3 = act(F1(), e3, AF.Identity, float(MID - 1), delta)
+    val = new("aH", 256)
+    act(sub(val, 16, 240), sub(base, 16, 240), AF.Identity, 1.0, delta)
+    act(sub(val, 0, 16), sub(base, 0, 16), AF.Identity, n3, z3)
+    act(sub(val, 240, 256), sub(base, 240, 256), AF.Identity, n1, z1)
+    lbk = [act(F1(), iF, AF.Identity, bias=16.0 + 16 * k) for k in range(5)]
     fill(V("zt", 0, 512), 0.0)
-    quant(V("zq", 0, 128), V("zs", 0, 128), V("zt", 0, 512))
-    dma("y", V("laq", 0, Z0), V("zq", 0, Z0), "dz0", True)
-    dma("y", V("las", 0, Z0), V("zs", 0, Z0), "dz1")
-    for a, b in ((0, 512), (512, 1024)):
-        quant(V("wq", a, b), V("ws", a, b), V("wt", 4 * a, 4 * b))
-    off_t = ts(new("aU", 8), t_g, 15.0, ADD)
-    off_g = ts(new("aU", 8), t_g, iF, ADD)
-    low8 = ts(F1(), iF, 7.5, A.is_gt, 56.0, MUL)
-    ln = ts(F1(), tt(F1(), low8, iF, ADD), 1.5, ADD)
-    npt = tt(new("aF", 256), np1, np2, ADD)
-    hl = ts(F1(), iF, 14.5, LT, 1024.0, MUL)
-    hr = ts(F1(), iF, 0.5, A.is_gt, float(1 << 20), MUL)
-    m0 = tt(F1(), ts(F1(), hl, -1.0, MUL, -1.0, ADD), lo, MUL)
-    m3 = tt(F1(), tt(F1(), hr, hl, SUB), lo, MUL)
+    if r == 0:
+        fill(V("xt", 0, 64), 0.0)
+    quant("gr", 16 if r else 0, 272, "xt", 64 if r else 0)
+    a = 288 if r < N - 1 else 272
+    quant("gr", a, a + 128, "zt", 0)
+    XS = fill(new("aH", 32), 1000.0)
+    alpha = fill(new("aH", 128), 1.0 / 32)
 
-    ab = act(new("aH", 128), V("sg", 0, 128), AF.Abs)
-    tt(sub(M, 1, 128), V("sg", 0, 127), V("sg", 1, 128), MUL)
-    v1 = tt(new("aH", 128), sub(M, 0, 128), sub(M, 1, 129), MIN)
-    v2 = tt(new("aH", 128), v1, ab, MIN)
-    av = ts(new("aH", 128), v2, 17.0, LT)
-    scan(sub(X, 1, 129), d0, av, one0)
+    SV, X = new("aH", 128), new("aH", 128)
+    sg = V("sg", 0, 128)
+    act(sub(SV, 0, 127), sub(sg, 1, 128), AF.Sign)
+    st = scan(new("aH", 128), alpha, sg, sub(sg, 0, 1))
+    ts(sub(SV, 127, 128), sub(sg, 127, 128), 1.0 / 18, MUL)
+    pr = tt(new("aH", 128), st, SV, MUL)
+    av = ts(new("aH", 128), pr, 18.0, LT)
+    scan(X, d0, av, one0)
 
-    Y = gather(new("aH", 96), X, off_y)
-    ZR = tr(new("aH", 128), sub(X, 1, 129))
-    YT = tr(new("aH", 96), Y)
-    SR = scan(new("aF", 128), rs, ZR)
-    TG = gather(new("aF", 128), SR, off_t, "s")
-    S6 = scan(new("aF", 96), sub(rs, 0, 96), YT)
-    V6 = tt(new("aI", 96), S6, YT, MUL)
-    VR = tt(new("aI", 128), SR, ZR, MUL)
-    A6 = ts(new("aI", 96), V6, 56 | 1 << 20, A.bitwise_and)
-    AR = ts(new("aI", 128), VR, 56 | 1 << 20, A.bitwise_and)
-    E6 = ts(new("aH", 96), A6, ge, EQ)
-    ts(sub(E, 0, 128), AR, float((1 << 20) + 56 - 8 * r), EQ)
-    a1 = tt(new("aH", 16), sub(E6, 16, 32), sub(E6, 80, 96), MAX)
-    a2 = tt(new("aH", 16), sub(E6, 47, 63), sub(E6, 49, 65), MAX)
-    a3 = tt(new("aH", 16), a1, sub(E6, 48, 64), MAX)
-    nd = tt(new("aF", 16), a3, a2, MAX)
-    tot = total(F1(), nd)
-    pre = scan(new("aF", 16), sub(ones, 0, 16), nd)
-    mt = ts(new("aF", 32), mk, tot, MUL)
-    q2 = tt(new("aF", 16), nd, trash, MUL)
-    mtt = tr(new("aF", 32), mt)
-    q1 = tt(new("aF", 16), trash, pre, SUB)
-    base = total(F1(), mtt)
-    q3 = tt(new("aF", 16), q1, q2, SUB)
-    off = ts(new("aU", 16), q3, base, ADD)
+    Y = gather(new("aH", 32), X, off_y)
+    act(sub(XS, 0, 8), sub(X, 15, 128, 16), AF.Copy)
+    YT = tr(new("aH", 32), Y)
+    S6 = scan(new("aF", 32), rs, YT)
+    V6 = tt(new("aI", 16), sub(S6, 16, 32), sub(YT, 16, 32), MUL)
+    A6 = ts(new("aI", 16), V6, 127 | 1 << 20, A.bitwise_and)
+    o6 = tt(new("aF", 16), A6, trash, MAX)
+    off = ts(new("aU", 16), o6, float((1 << 20) - 256), SUB)
     run("v", [win], [off, val], lambda e: e.tensor_copy(ap(win).indirect(ap(off)), ap(val)))
-    D = gather(new("aH", 128), sub(win, 0, 64), off_d)
-    DT = new("aH", 256)
-    tr(sub(DT, 0, 128), D)
-    tr(sub(DT, 128, 256), D)
-    lc = new("aH", 32)
-    for a in range(4):
-        o, i = sub(lc, 8 * a, 8 * a + 8, 1, 0, 32), sub(DT, 0, 256, 36, 32 * a, 32 * a + 32)
-        if a % 2:
-            run("s", [o], [i], lambda e: e.activation(ap(o), ap(i), AF.Copy))
-        else:
-            cp(o, i)
-    cp(sub(lc, 0, 32, 1, 32, 64), sub(lc, 0, 32, 1, 0, 32))
-    lw = new("aU", 32)
-    cp(sub(lw, 0, 32, 1, 0, 64), sub(lc, 0, 32, 1, 0, 64))
-    cp(sub(lw, 0, 32, 1, 64, 128), sub(lc, 0, 32, 1, 0, 64))
+    D = gather(new("aH", 256), win, off_d)
+    DT = tr(new("aH", 256), D)
+    lw = new("aU", 48)
+    run("v", [lw], [DT, off_l], lambda e: e.tensor_scalar(ap(lw), ap(DT).indirect(ap(off_l)), float(MID), None, ADD))
 
-    xq, xs = V("xq", 0, 256), V("xs", 0, 256)
-    for a, b in ((0, r), (r + 1, N)):
-        if a < b:
-            pickc(V("slq", 64 * a, 64 * b), xq, sub(lw, 4 * a, 4 * b))
-            gather(V("sls", 64 * a, 64 * b), xs, sub(lw, 4 * a, 4 * b), "s")
-    home = lambda n: V(n, Z0 + 64 * r, Z0 + 64 * r + NC)
-    slot = lambda n, k: V(n, 64 * k, 64 * k + NC)
-    send([(k, slot("slq", k), home("laq")) for k in others], True, "rlc", "lland", [slot("slq", k) for k in others])
-    send([(k, slot("sls", k), home("las")) for k in others], False, "rls", "lland", [slot("sls", k) for k in others])
-    for k in others:
-        for n, m in (("laq", "rlc"), ("las", "rls")):
-            note(V(n, Z0 + 64 * k, Z0 + 64 * k + NC), True, None, m, count[m], {})
+    gq, gs = V("grq", 0, 304), V("grs", 0, 304)
+    pickc(V("slq", 0, NC * 7), gq, sub(lw, 6, 41))
+    gather(V("sls", 0, NC * 7), gs, sub(lw, 6, 41), "s")
+    home = lambda n, k: V(n, SL * k + 16, SL * k + SL)
+    slot = lambda n, i: V(n, NC * i, NC * i + NC)
+    for n, bits, m in (("q", True, "rlc"), ("s", False, "rls")):
+        send([(k, slot("sl" + n, i), home("la" + n, r)) for i, k in enumerate(others)], 1, bits, m, "lland",
+             [slot("sl" + n, i) for i in range(7)], N - 1)
+        for k in others:
+            note(home("la" + n, k), True, None, m, count[m], {})
 
-    nb = act(new("aF", 8), t_nb, AF.Identity, bias=ln)
-    TF = tr(new("aF", 128), TG)
-    acc = new("aF", 8)
-    for c in range(8):
-        act(new("aH", 128), TF, AF.Sign, -1.0, sub(nb, c, c + 1), sub(acc, c, c + 1))
-    H1 = tt(new("aH", 127), sub(E, 0, 127), sub(E, 2, 129), MAX)
-    w1 = tt(new("aF", 128), VR, sub(E, 0, 128), MUL)
-    H2 = tt(new("aH", 127), H1, sub(E, 1, 128), MAX)
-    w2 = new("aF", 128)
-    tt(sub(w2, 1, 128), sub(w1, 1, 128), H2, SUB)
-    wd = gather(new("aF", 128), sub(w2, 16, 128), off_g)
-    tr(sub(tv, 0, 128), wd)
-    dn = act(new("aF", 128), sub(r16, 0, 128), AF.Copy, scale=lo)
-    bt = act(new("aF", 128), st0, AF.Copy, scale=one0)
-    ts(sub(ec, 1, 129), sub(tv, 0, 128), -1.5, LT)
-    nh = ts(new("aH", 128), sub(tv, 0, 128), -0.5, LT)
-    h1 = tt(new("aH", 128), sub(ec, 0, 128), sub(ec, 2, 130), MAX)
-    h2 = tt(new("aH", 128), h1, nh, MAX)
-    h3 = tt(new("aF", 128), h2, bt, ADD)
-    rp = new("aU", 16)
-    ts(sub(rp, 0, 16, 2), acc, 0.5, MUL, 64.0, ADD)
-    ts(sub(rp, 1, 16, 2), acc, 0.5, MUL, 64.0, ADD)
-    ov = gather(new("aF", 256), tv, rp, "s")
-    xn = scan(new("aF", 128), dn, h3)
-    zn = tr(new("aF", 128), xn)
-    sn = scan(new("aF", 128), rs, zn)
-    pd = gather(new("aF", 128), sub(sn, 16, 128), off_g)
-    tr(sub(pc, 1, 129), pd)
-    p1 = act(new("aF", 128), sub(pc, 1, 129), AF.Identity, m0, m3)
-    p2 = act(new("aF", 128), sub(pc, 0, 128), AF.Copy, m1)
-    p3 = ts(new("aF", 128), sub(pc, 2, 130), m2, MUL)
-    quant(V("wq", 1024, 1280), V("ws", 1024, 1280), V("wt", 4096, 5120))
-    p4 = tt(new("aF", 128), p1, p3, ADD)
-    tt(sub(pt, 0, 128), p4, p2, ADD)
-    gp = gather(new("aF", 256), pt, rp, "s")
-    oh = tt(new("aF", 256), ov, npt, EQ)
-    pickc(V("laq", Z0 + 64 * r, Z0 + 64 * r + 64), xq, sub(lw, 4 * r, 4 * r + 4))
-    gather(V("las", Z0 + 64 * r, Z0 + 64 * r + 64), xs, sub(lw, 4 * r, 4 * r + 4), "s")
-    op = tt(new("aF", 256), oh, gp, MUL)
-    ot = tr(new("aF", 256), op)
-    os_ = scan(new("aF", 256), r16, ot)
-    ab2 = cp(new("aI", 16), sub(os_, 15, 256, 16))
-    va, vb = sub(ab2, 0, 16, 2), sub(ab2, 1, 16, 2)
-    li, lu = new("aI", 40), new("aU", 40)
-    k0 = ts(sub(li, 0, 8), va, 1023, A.bitwise_and)
-    ts(sub(li, 8, 16), vb, 1023, A.bitwise_and)
-    ts(sub(li, 16, 24), vb, 10, A.arith_shift_right)
-    ts(sub(li, 24, 32), va, 10, A.arith_shift_right, 1023, A.bitwise_and)
-    fr = ts(new("aI", 8), va, 20, A.arith_shift_right)
-    kr = ts(new("aI", 8), k0, 1.0, ADD)
-    cp(sub(lu, 0, 32), sub(li, 0, 32))
-    tt(sub(li, 32, 40), kr, fr, MUL)
-    cp(sub(lu, 32, 40), sub(li, 32, 40))
+    XT = tr(new("aH", 32), XS)
+    C = total(F1(), sub(XT, 0, 16))
+    npt = tt(new("aF", 256), np1, np2, ADD)
+    ind = ts(new("aH", 256), npt, C, GE)
+    it = tr(new("aH", 256), ind)
+    pickc(V("laq", SL * r, SL * r + SL), gq, sub(lw, 0, 6))
+    gather(V("las", SL * r, SL * r + SL), gs, sub(lw, 0, 6), "s")
+    iq = scan(new("aH", 256), r32, it)
+    lu = new("aU", 40)
+    for k in range(5):
+        ts(sub(lu, 8 * k, 8 * k + 8), sub(iq, 31, 256, 32), float(SL), MUL, lbk[k], ADD)
+    quant("la", SL * N + 16, LW, "zt", 0)
+    for a, b in ((0, 512), (512, 1024), (1024, 1280)):
+        quant("w", a, b, "wt", 4 * a)
 
     tk = lambda n, k: V(n, 128 * k, 128 * k + 128)
     lk = lambda k: sub(lu, 8 * k, 8 * k + 8)
     for k in range(5):
         pickc(tk("tq", k), V("laq", 0, LW), lk(k))
     for k in range(5):
-        gather(tk("ts", k), V("las", 0, LW), lk(k), "v" if k > 3 else "s")
+        gather(tk("ts", k), V("las", 0, LW), lk(k), "v" if k % 2 else "s")
     for k in range(5):
         for o in (0, 1):
-            a = 128 * (2 * k + o)
+            a = 128 * (2 * KW[k] + o)
             mm(V("ps", 1024 + 512 * o, 1152 + 512 * o), V("wq", a, a + 128), V("ws", a, a + 128), tk("tq", k), tk("ts", k), k == 0, k == 4)
     cp(V("yo", 0, 128), V("ps", 1024, 1152))
     act(V("yo", 128, 256), V("ps", 1536, 1664), AF.Copy)

@@ -12,12 +12,12 @@ KW = (1, 3, 0, 4, 2)
 F8, U8, BF, F32 = "float8_e4m3fn_x4", "uint8", "bfloat16", "float32"
 SCRATCH = {"aF": ("sbuf", [128, 4096], F32), "aH": ("sbuf", [128, 6144], BF), "aI": ("sbuf", [128, 256], "int32"),
            "aU": ("sbuf", [128, 512], "uint16"), "sg": ("sbuf", [128, 128], BF), "xt": ("sbuf", [128, 1088], BF),
-           "uc": ("sbuf", [128, 16], BF), "ut": ("sbuf", [128, 512], BF), "wt": ("sbuf", [128, 5120], BF), "zt": ("sbuf", [128, 512], BF),
+           "uc": ("sbuf", [128, 16], BF), "ut": ("sbuf", [128, 512], BF), "wt": ("sbuf", [128, 5120], BF), "zt": ("sbuf", [128, 640], BF),
            "yo": ("sbuf", [128, 256], F32), "ps": ("psum", [128, 2048], F32)}
-for _n, _w in (("x", 256), ("u", 128), ("w", 1280), ("gr", PW), ("sl", NC * 7), ("la", LW), ("t", 640)):
+for _n, _w in (("e", 128), ("u", 128), ("w", 1280), ("gr", PW), ("sl", NC * 7), ("la", LW), ("t", 640)):
     SCRATCH[_n + "q"] = ("sbuf", [128, _w], F8)
     SCRATCH[_n + "s"] = ("sbuf", [128, _w], U8)
-DMAS = ["dx0", "dx1", "du", "dw0", "dw1", "dw2", "dy0", "dy1"]
+DMAS = ["de0", "de1", "dx0", "dx1", "du", "dw0", "dw1", "dw2", "dy0", "dy1"]
 SEMAPHORES = ["qv", "qs", "qt", "qg"] + DMAS + ["rsign", "lsign", "rhc", "rhs", "lhalo", "rlc", "rls", "lland"]
 A = AluOpType
 AF = ActivationFunctionType
@@ -125,8 +125,8 @@ def rank_program(g, core, T, topo):
         run("v", [o], [], lambda e: e.memset(ap(o), c))
         return o
 
-    def total(o, i):
-        run("v", [o], [i], lambda e: e.tensor_reduce(ap(o), ap(i), AX, ADD))
+    def minus_total(o, i):
+        run("v", [o], [i], lambda e: e.tensor_reduce(ap(o), ap(i), AX, ADD, negate=True))
         return o
 
     def gather(o, win, off, q="v"):
@@ -169,9 +169,7 @@ def rank_program(g, core, T, topo):
         if not start:
             note(o, True, "t", "qt", count["qt"], dict(known["t"]))
 
-    others = [d for d in range(N) if d != r]
-
-    def send(pairs, width, bits, rsem, lsem, ins, senders):
+    def send(pairs, width, bits, rsem, lsem, ins, arrive):
         sync("g", [], ins)
         xs = []
         for k, (d, src, dst) in enumerate(pairs):
@@ -185,68 +183,70 @@ def rank_program(g, core, T, topo):
                                         remote_sem=T.sem[rsem], src=a, dst=b))
         g.remote_dma_fused(xs, local_sem=T.sem[lsem])
         count[lsem] = count.get(lsem, 0) + width * len(xs)
-        count[rsem] = count.get(rsem, 0) + width * senders
+        count[rsem] = count.get(rsem, 0) + arrive
 
     F1 = lambda: new("aF", 1)
-    dma("s", V("uc", 0, 8), T.u[:, 0:8], "du")
-    dma("y", V("xt", 64, 576), T.x[:, 0:512], "dx0")
-    dma("s", V("xt", 576, 1088), T.x[:, 512:1024], "dx1")
-    for k, (a, b) in enumerate(((0, 2048), (2048, 4096), (4096, 5120))):
-        dma("y", V("wt", a, b), T.w[:, a:b], "dw%d" % k)
+    turn = 1 if r % 2 == 0 else -1
+    order = [d for b in range(0, N, 2) for d in ((r + b) % N, (r + b) % N + turn)]
+    others = order[1:]
+
+    dma("y", V("uc", 0, 8), T.u[:, 0:8], "du")
+    dma("s", V("zt", 64, 128), T.x[:, 960:1024], "de1")
+    dma("y", V("zt", 0, 64), T.x[:, 0:64], "de0")
+    dma("s", V("xt", 64, 576), T.x[:, 0:512], "dx0")
+    dma("y", V("xt", 576, 1088), T.x[:, 512:1024], "dx1")
 
     lane = iota(new("aI", 1), [[0, 1]], 0, 1)
-    jj = iota(new("aF", 64), [[0, 4], [1, 16]])
-    t_y = const(new("aF", 2), 16 * r)
-    t_d = new("aF", 16)
-    iota(sub(t_d, 0, 2), [[0, 2]], 383 - 8 * r)
-    if r > 0:
-        iota(sub(t_d, 2, 2 + 2 * r), [[-8, r], [0, 2]], 383)
-    if r < N - 1:
-        iota(sub(t_d, 2 + 2 * r, 16), [[-8, N - 1 - r], [0, 2]], 383 - 8 * (r + 1))
-    t_l = iota(new("aF", 3), [[16, 3]], -1)
-    t_tr = iota(new("aF", 16), [[1, 16]], (1 << 20) - 256)
-    np1 = iota(new("aF", 256), [[128, 8], [0, 4], [1, 8]], 8 * r + 1)
+    jj = iota(new("aH", 64), [[0, 4], [1, 16]])
     ones = fill(new("aH", 128), 1.0)
-    bF = cp(F1(), ts(new("aI", 1), lane, 31, A.bitwise_and))
-    w = act(F1(), bF, AF.Abs, bias=-15.5)
-    first = act(F1(), w, AF.Relu, bias=-14.5)
-    last = act(F1(), w, AF.Relu, -1.0, 1.5)
-    last2 = act(F1(), w, AF.Relu, -1.0, 2.5)
-    c0 = act(F1(), last, AF.Identity, 0.0625, act(F1(), first, AF.Identity, -0.0625, 0.0625))
-    c1 = act(F1(), first, AF.Identity, -8.0, 16.0)
-    d = ts(new("aF", 64), jj, w, ADD, -15.5, ADD)
-    f3 = ts(new("aF", 64), d, 2.0, EQ, 1024.0, MUL)
-    f4 = ts(new("aF", 64), d, 3.0, GE)
-    f1 = ts(new("aF", 64), d, 0.0, EQ, c0, MUL)
-    f2 = ts(new("aF", 64), d, 1.0, EQ, c1, MUL)
-    f34 = tt(new("aF", 64), f3, f4, ADD)
-    f12 = tt(new("aF", 64), f1, f2, ADD)
+    bI = ts(new("aI", 1), lane, 31, A.bitwise_and)
+    bm = ts(F1(), bI, -15.5, ADD)
+    w = act(F1(), bm, AF.Abs)
+    half = act(new("aF", 16), sub(ones, 0, 16), AF.Copy, 1.0 / 36)
+    fill(V("zt", 128, 640), 0.0)
+    first = ts(F1(), w, 15.0, GE, -0.0625, MUL)
+    q0 = ts(F1(), w, 15.9375, MUL, 0.0625 - 15.9375 * 15.5, ADD)
+    cut = tt(F1(), first, q0, ADD)
     ft = new("aH", 256)
-    tt(sub(ft, 0, 64), f12, f34, ADD)
+    f1 = ts(new("aH", 64), jj, 15.9375, MUL, cut, ADD)
+    ts(sub(ft, 0, 64), f1, 0.0, MAX, 16.0, MIN)
+    eq = scan(new("aF", 16), sub(ft, 0, 16), half)
+    nrm = F1()
 
-    for t in (0, 1):
-        ts(V("ut", t, 512, 4), ones, V("uc", t, t + 1), MUL)
-    for t in (2, 3):
-        act(V("ut", t, 512, 4), ones, AF.Identity, 0.0, V("uc", t, t + 1))
-    for a in (64, 128, 192):
-        act(sub(ft, a, a + 64), sub(ft, 0, 64), AF.Copy)
-    e = 2.0 / 1024
-    nrm = act(F1(), first, AF.Identity, e, act(F1(), last, AF.Identity, 28.0 + e, act(F1(), last2, AF.Identity, 2.0 - e, e)))
-    quant("u", 0, 128, "ut", 0)
-    sgn, cells = new("aH", 256), new("aH", 256)
-    for h in (0, 1):
-        quant("x", 128 * h, 128 * h + 128, "xt", 64 + 512 * h)
-        mm(V("ps", 512 * h, 512 * h + 128), V("uq", 0, 128), V("us", 0, 128),
-           V("xq", 128 * h, 128 * h + 128), V("xs", 128 * h, 128 * h + 128), True, True)
-    halo = [(k, a, b) for k, a, b in ((r + 1, 240, 0), (r - 1, 0, 272)) if 0 <= k < N]
-
-    def edges(n, bits, rsem):
+    halo = [(k, a, b) for k, a, b in ((r + 1, 16, 0), (r - 1, 0, 272)) if 0 <= k < N]
+    wide = lambda k: 8 // sum(0 <= j < N for j in (k - 1, k + 1))
+    quant("e", 0, 128, "zt", 0)
+    for n, bits, rsem in (("q", True, "rhc"), ("s", False, "rhs")):
         at = lambda m, a: V(m + n, a, a + 16)
-        send([(k, at("x", a), at("gr", b)) for k, a, b in halo], 4, bits, rsem, "lhalo", [at("x", a) for k, a, b in halo], len(halo))
+        send([(k, at("e", a), at("gr", b)) for k, a, b in halo], wide(r), bits, rsem, "lhalo",
+             [at("e", a) for k, a, b in halo], sum(wide(k) for k, a, b in halo))
         for k, a, b in halo:
             note(at("gr", 0 if k < r else 272), True, None, rsem, count[rsem], {})
+    t_e = iota(new("aF", 2), [[2, 2]], 1)
+    t_y = const(new("aF", 2), 16 * r)
+    t_l = iota(new("aF", 3), [[16, 3]], -1)
+    t_d = new("aF", 8)
+    nb = (N - r + 1) // 2
+    iota(sub(t_d, 0, 2 * nb), [[-16, nb], [0, 2]], 383 - 8 * r)
+    if nb < 4:
+        iota(sub(t_d, 2 * nb, 8), [[-16, 4 - nb], [0, 2]], 383 - 8 * ((r + 2 * nb) % N))
 
-    edges("q", True, "rhc")
+    for t in (1, 2, 3):
+        act(V("ut", t, 512, 4), ones, AF.Identity, 0.0, V("uc", t, t + 1))
+    ts(V("ut", 0, 512, 4), ones, V("uc", 0, 1), MUL)
+    for a in (64, 128, 192):
+        act(sub(ft, a, a + 64), sub(ft, 0, 64), AF.Copy)
+    if r == 0:
+        fill(V("xt", 0, 64), 0.0)
+    sgn, cells = new("aH", 256), new("aH", 256)
+    for h in (0, 1):
+        a = 0 if r == 0 and h == 0 else 16 + 128 * h
+        quant("gr", a, 144 + 128 * h, "xt", 4 * a)
+        if h == 0:
+            quant("u", 0, 128, "ut", 0)
+        a = 16 + 128 * h
+        mm(V("ps", 512 * h, 512 * h + 128), V("uq", 0, 128), V("us", 0, 128), V("grq", a, a + 128), V("grs", a, a + 128), True, True)
+    run("v", [nrm], [sub(eq, 15, 16)], lambda e: e.reciprocal(ap(nrm), ap(sub(eq, 15, 16))))
     for h in (0, 1):
         ts(sub(sgn, 128 * h, 128 * h + 128), V("ps", 512 * h, 512 * h + 128), 0.0, A.is_gt, -0.5, ADD)
     scan(cells, ft, sgn)
@@ -255,62 +255,65 @@ def rank_program(g, core, T, topo):
     send([(k, own, own) for k in others], 1, False, "rsign", "lsign", [own], N - 1)
     for k in others:
         note(V("sg", 16 * k, 16 * k + 16), True, None, "rsign", count["rsign"], {})
-    edges("s", False, "rhs")
+    g.sync.wait_ge(T.sem["lsign"], count["lsign"])
+    known["y"]["lsign"] = count["lsign"]
+    for k, (a, b) in enumerate(((0, 2048), (2048, 4096), (4096, 5120))):
+        dma("y", V("wt", a, b), T.w[:, a:b], "dw%d" % k)
 
+    t_tr = iota(new("aF", 16), [[1, 16]], (1 << 20) - 256)
     base = iota(new("aH", 256), [[-1, 16], [16, 16]], 31 - MID)
-    win = const(new("aH", 384), MID)
     onef = const(new("aF", 32), 1)
     rs = asel(new("aF", 32), asel(new("aF", 32), onef, [[1, 32]], NE, 0.0, 0), [[1, 32]], NE, -1.0, -16)
-    np2 = iota(new("aF", 256), [[0, 16], [64, 2], [0, 8]])
+    win = const(new("aH", 384), MID)
+    XS = const(new("aH", 32), 1000)
+    npt = new("aF", 256)
+    for a in range(8):
+        iota(sub(npt, 32 * a, 32 * a + 32), [[0, 2], [128, 2], [2, 8]], 256 * a + 16 * r + 3)
     r32 = asel(new("aH", 256), const(new("aH", 256), 1), [[0, 8], [1, 32]], NE, 0.0, 0)
 
-    lo = ts(F1(), bF, 16.0, LT)
-    one0 = ts(F1(), bF, 0.0, EQ)
-    iF = cp(F1(), ts(new("aI", 1), lane, 15, A.bitwise_and))
-    high = ts(F1(), iF, 8.0, GE, -56.0, MUL)
-    e1, n1 = ts(F1(), bF, 1.0, EQ), ts(F1(), bF, 1.0, NE)
-    e3, n3 = ts(F1(), bF, 3.0, EQ), ts(F1(), bF, 3.0, NE)
-    off_y = ts(new("aU", 2), t_y, iF, ADD)
-    sl8 = tt(F1(), high, iF, SUB)
-    la = ts(new("aF", 3), t_l, iF, ADD, 0.0, MAX)
-    lb = ts(new("aI", 3), la, 0.2, MUL, -0.4, ADD)
-    off_d = ts(new("aU", 16), t_d, sl8, ADD)
-    lc = ts(new("aF", 3), lb, 27.0, MUL)
-    ld = tt(new("aF", 3), lc, la, ADD)
-    off_l = ts(new("aU", 3), ld, 255.0, MIN)
+    alpha = act(new("aH", 128), ones, AF.Copy, scale=1.0 / 32)
+    lo = ts(F1(), bm, 0.0, LT)
+    one0 = ts(F1(), bm, -15.5, EQ)
+    iF = ts(F1(), ts(new("aI", 1), lane, 15, A.bitwise_and), 0.0, ADD)
     d0 = act(new("aH", 128), ones, AF.Copy, scale=lo)
+    hb = act(F1(), bm, AF.Identity, 0.5 * turn, 7.75 * turn)
+    s1 = act(F1(), iF, AF.Identity, 1.0 - 0.5 * turn, hb)
+    off_y = ts(new("aU", 2), t_y, iF, ADD)
+    high = ts(F1(), iF, 8.0, GE, 56.0, MUL)
+    la = ts(new("aF", 3), t_l, iF, ADD, 39.0, MIN)
+    lb = ts(new("aI", 3), la, 0.2, MUL, -0.4, ADD)
+    e13 = ts(new("aF", 2), t_e, iF, EQ)
+    n13 = ts(new("aF", 2), t_e, iF, NE)
+    lc = ts(new("aF", 3), lb, 11.0, MUL)
+    off_d = ts(new("aU", 8), t_d, s1, SUB, high, SUB)
+    ld = tt(new("aF", 3), lc, la, ADD)
+    off_l = ts(new("aU", 3), ld, 0.0, MAX)
+    quant("gr", 288 if r < N - 1 else 272, 416 if r < N - 1 else 400, "zt", 128)
+    quant("la", SL * N + 16, LW, "zt", 128)
     i16 = act(F1(), iF, AF.Copy, scale=16.0)
     trash = act(new("aF", 16), t_tr, AF.Identity, bias=i16)
-    sx = act(F1(), bF, AF.Identity, bias=-2.0)
+    sx = act(F1(), iF, AF.Identity, bias=-2.0)
     sx2 = act(F1(), sx, AF.Square)
     delta = act(F1(), act(F1(), sx2, AF.Identity, 7.0 / 3, -4.0 / 3), AF.Copy, scale=sx)
-    z1 = act(F1(), e1, AF.Identity, float(MID + 1), delta)
-    z3 = act(F1(), e3, AF.Identity, float(MID - 1), delta)
+    z1 = act(F1(), sub(e13, 0, 1), AF.Identity, float(MID + 1), delta)
+    z3 = act(F1(), sub(e13, 1, 2), AF.Identity, float(MID - 1), delta)
     val = new("aH", 256)
     act(sub(val, 16, 240), sub(base, 16, 240), AF.Identity, 1.0, delta)
-    act(sub(val, 0, 16), sub(base, 0, 16), AF.Identity, n3, z3)
-    act(sub(val, 240, 256), sub(base, 240, 256), AF.Identity, n1, z1)
-    lbk = [act(F1(), iF, AF.Identity, bias=16.0 + 16 * k) for k in range(5)]
-    fill(V("zt", 0, 512), 0.0)
-    if r == 0:
-        fill(V("xt", 0, 64), 0.0)
-    quant("gr", 16 if r else 0, 272, "xt", 64 if r else 0)
-    a = 288 if r < N - 1 else 272
-    quant("gr", a, a + 128, "zt", 0)
-    XS = fill(new("aH", 32), 1000.0)
-    alpha = fill(new("aH", 128), 1.0 / 32)
+    act(sub(val, 0, 16), sub(base, 0, 16), AF.Identity, sub(n13, 1, 2), z3)
+    act(sub(val, 240, 256), sub(base, 240, 256), AF.Identity, sub(n13, 0, 1), z1)
 
     SV, X = new("aH", 128), new("aH", 128)
     sg = V("sg", 0, 128)
     act(sub(SV, 0, 127), sub(sg, 1, 128), AF.Sign)
     st = scan(new("aH", 128), alpha, sg, sub(sg, 0, 1))
-    ts(sub(SV, 127, 128), sub(sg, 127, 128), 1.0 / 18, MUL)
+    ts(sub(SV, 127, 128), sub(sg, 127, 128), -1.0, MAX, 1.0, MIN)
     pr = tt(new("aH", 128), st, SV, MUL)
     av = ts(new("aH", 128), pr, 18.0, LT)
     scan(X, d0, av, one0)
 
     Y = gather(new("aH", 32), X, off_y)
     act(sub(XS, 0, 8), sub(X, 15, 128, 16), AF.Copy)
+    lbk = [act(F1(), iF, AF.Identity, bias=16.0 + 16 * k + 16 * SL) for k in range(5)]
     YT = tr(new("aH", 32), Y)
     S6 = scan(new("aF", 32), rs, YT)
     V6 = tt(new("aI", 16), sub(S6, 16, 32), sub(YT, 16, 32), MUL)
@@ -318,43 +321,45 @@ def rank_program(g, core, T, topo):
     o6 = tt(new("aF", 16), A6, trash, MAX)
     off = ts(new("aU", 16), o6, float((1 << 20) - 256), SUB)
     run("v", [win], [off, val], lambda e: e.tensor_copy(ap(win).indirect(ap(off)), ap(val)))
-    D = gather(new("aH", 256), win, off_d)
-    DT = tr(new("aH", 256), D)
+    D = gather(new("aH", 128), win, off_d)
+    DT = tr(new("aH", 128), D)
     lw = new("aU", 48)
     run("v", [lw], [DT, off_l], lambda e: e.tensor_scalar(ap(lw), ap(DT).indirect(ap(off_l)), float(MID), None, ADD))
 
     gq, gs = V("grq", 0, 304), V("grs", 0, 304)
-    pickc(V("slq", 0, NC * 7), gq, sub(lw, 6, 41))
-    gather(V("sls", 0, NC * 7), gs, sub(lw, 6, 41), "s")
     home = lambda n, k: V(n, SL * k + 16, SL * k + SL)
     slot = lambda n, i: V(n, NC * i, NC * i + NC)
-    for n, bits, m in (("q", True, "rlc"), ("s", False, "rls")):
-        send([(k, slot("sl" + n, i), home("la" + n, r)) for i, k in enumerate(others)], 1, bits, m, "lland",
-             [slot("sl" + n, i) for i in range(7)], N - 1)
-        for k in others:
-            note(home("la" + n, k), True, None, m, count[m], {})
+    for a, b in ((4, 7), (0, 4)):
+        pickc(V("slq", NC * a, NC * b), gq, sub(lw, 6 + 5 * a, 6 + 5 * b))
+        gather(V("sls", NC * a, NC * b), gs, sub(lw, 6 + 5 * a, 6 + 5 * b), "s")
+    for n, bits, m, a, b, width in (("q", True, "rlc", 4, 7, 2), ("q", True, "rlc", 0, 4, 2), ("s", False, "rls", 0, 7, 1)):
+        send([(others[i], slot("sl" + n, i), home("la" + n, r)) for i in range(a, b)], width, bits, m, "lland",
+             [slot("sl" + n, i) for i in range(a, b)], width * (N - 1) if a == 0 else 0)
+        if a == 0:
+            for k in others:
+                note(home("la" + n, k), True, None, m, count[m], {})
 
     XT = tr(new("aH", 32), XS)
-    C = total(F1(), sub(XT, 0, 16))
-    npt = tt(new("aF", 256), np1, np2, ADD)
-    ind = ts(new("aH", 256), npt, C, GE)
-    it = tr(new("aH", 256), ind)
+    C = minus_total(F1(), sub(XT, 0, 16))
+    ind = act(new("aH", 256), npt, AF.Sign, 0.5, C)
     pickc(V("laq", SL * r, SL * r + SL), gq, sub(lw, 0, 6))
     gather(V("las", SL * r, SL * r + SL), gs, sub(lw, 0, 6), "s")
+    quant("w", 0, 512, "wt", 0)
+    it = tr(new("aH", 256), ind)
     iq = scan(new("aH", 256), r32, it)
-    lu = new("aU", 40)
+    lf, lu = new("aF", 40), new("aU", 40)
     for k in range(5):
-        ts(sub(lu, 8 * k, 8 * k + 8), sub(iq, 31, 256, 32), float(SL), MUL, lbk[k], ADD)
-    quant("la", SL * N + 16, LW, "zt", 0)
-    for a, b in ((0, 512), (512, 1024), (1024, 1280)):
+        act(sub(lf, 8 * k, 8 * k + 8), sub(iq, 31, 256, 32), AF.Identity, SL / 2.0, lbk[k])
+    for a, b in ((512, 1024), (1024, 1280)):
         quant("w", a, b, "wt", 4 * a)
+    ts(lu, lf, 0.0, ADD)
 
     tk = lambda n, k: V(n, 128 * k, 128 * k + 128)
     lk = lambda k: sub(lu, 8 * k, 8 * k + 8)
     for k in range(5):
         pickc(tk("tq", k), V("laq", 0, LW), lk(k))
     for k in range(5):
-        gather(tk("ts", k), V("las", 0, LW), lk(k), "v" if k % 2 else "s")
+        gather(tk("ts", k), V("las", 0, LW), lk(k), "ssvsv"[k])
     for k in range(5):
         for o in (0, 1):
             a = 128 * (2 * KW[k] + o)

from concourse.bass import DstId, RemoteDMATransfer
from concourse.mybir import dt, AluOpType, ActivationFunctionType, AxisListType

N = 8
NS = 16
NC = 5 * NS
SL = NC + 16
LW = SL * N + 16 + 128
PW = 16 + 256 + 16 + 128
MID = 144
KW = (1, 3, 0, 4, 2)
F8, U8, BF, F32 = "float8_e4m3fn_x4", "uint8", "bfloat16", "float32"
SCRATCH = {"aF": ("sbuf", [128, 4096], F32), "aH": ("sbuf", [128, 6144], BF), "aI": ("sbuf", [128, 256], "int32"),
           "aU": ("sbuf", [128, 512], "uint16"), "sg": ("sbuf", [128, 128], BF), "xt": ("sbuf", [128, 1088], BF),
           "uc": ("sbuf", [128, 16], BF), "ut": ("sbuf", [128, 512], BF), "wt": ("sbuf", [128, 5120], BF), "zt": ("sbuf", [128, 640], BF),
           "yo": ("sbuf", [128, 256], F32), "ps": ("psum", [128, 2048], F32)}
for _n, _w in (("e", 128), ("u", 128), ("w", 1280), ("gr", PW), ("sl", NC * 7), ("la", LW), ("t", 640)):
    SCRATCH[_n + "q"] = ("sbuf", [128, _w], F8)
    SCRATCH[_n + "s"] = ("sbuf", [128, _w], U8)
DMAS = ["de0", "de1", "dx0", "dx1", "du", "dw0", "dw1", "dw2", "dy0", "dy1"]
SEMAPHORES = ["qv", "qs", "qt", "qg"] + DMAS + ["rsign", "lsign", "rhc", "rhs", "lhalo", "rlc", "rls", "lland"]
A = AluOpType
AF = ActivationFunctionType
AX = AxisListType.X
MUL, ADD, SUB, MAX, MIN = A.mult, A.add, A.subtract, A.max, A.min
EQ, NE, LT, GE = A.is_equal, A.not_equal, A.is_lt, A.is_ge


def rank_program(g, core, T, topo):
    r = T.rank_of(core)
    if r is None:
        return
    queues = {"v": g.vector, "s": g.scalar, "t": g.tensor, "g": g, "y": g.sync}
    csem = {"v": "qv", "s": "qs", "t": "qt", "g": "qg"}
    count = {}
    known = {q: {} for q in queues}
    hist = {}
    used = {"aF": 0, "aH": 0, "aI": 0, "aU": 0}
    unit = {"aF": 8, "aH": 16, "aI": 8, "aU": 16}

    def V(name, a, b, step=1):
        return (name, a, b, step)

    def new(arena, n):
        a = used[arena]
        used[arena] = a + -(-n // unit[arena]) * unit[arena]
        return V(arena, a, a + n)

    def sub(v, a, b, step=1):
        return V(v[0], v[1] + a, v[1] + b, step)

    def ap(v):
        return T[v[0]][:, v[1]:v[2]:v[3]] if v[3] != 1 else T[v[0]][:, v[1]:v[2]]

    def note(v, write, q, sem, val, clock):
        hist.setdefault(v[0], []).append((v, write, q, sem, val, clock))

    def sync(q, outs, ins):
        need = {}
        for group, out in ((outs, True), (ins, False)):
            for v in group:
                for (o, write, oq, sem, val, clock) in hist.get(v[0], []):
                    if not (write or out) or o[1] >= v[2] or v[1] >= o[2]:
                        continue
                    if not write and oq == q and sem == csem.get(q):
                        continue
                    if v[3] == o[3] and v[3] > 1 and (v[1] - o[1]) % v[3]:
                        continue
                    if val > need.get(sem, (0, None))[0]:
                        need[sem] = (val, clock)
        mine = csem.get(q)
        for sem in sorted(need, key=lambda s: (s == mine, s in DMAS, s)):
            val, clock = need[sem]
            if known[q].get(sem, 0) >= val:
                continue
            queues[q].wait_ge(T.sem[sem], val)
            for s2, v2 in list(clock.items()) + [(sem, val)]:
                known[q][s2] = max(known[q].get(s2, 0), v2)

    def run(q, outs, ins, call, sem=None, n=1):
        sync(q, outs, ins)
        sem = sem or csem[q]
        count[sem] = count.get(sem, 0) + n
        call(queues[q]).then_inc(T.sem[sem], n)
        clock = dict(known[q])
        for v in outs:
            note(v, True, q, sem, count[sem], clock)
        for v in ins:
            note(v, False, q, sem, count[sem], clock)

    def sc(s, ins):
        if isinstance(s, tuple):
            ins.append(s)
            return ap(s)
        return s

    def ts(o, i, s1, op0, s2=None, op1=None):
        ins = [i]
        a, b = sc(s1, ins), sc(s2, ins)
        if op1 is None:
            run("v", [o], ins, lambda e: e.tensor_scalar(ap(o), ap(i), a, None, op0))
        else:
            run("v", [o], ins, lambda e: e.tensor_scalar(ap(o), ap(i), a, b, op0, op1))
        return o

    def tt(o, a, b, op):
        run("v", [o], [a, b], lambda e: e.tensor_tensor(ap(o), ap(a), ap(b), op))
        return o

    def cp(o, i):
        run("v", [o], [i], lambda e: e.tensor_copy(ap(o), ap(i)))
        return o

    def tr(o, i):
        run("v", [o], [i], lambda e: e.transpose(ap(o), ap(i)))
        return o

    def scan(o, d0, d1, init=0.0):
        ins = [d0, d1]
        s = sc(init, ins)
        run("v", [o], ins, lambda e: e.tensor_tensor_scan(ap(o), ap(d0), ap(d1), s, MUL, ADD))
        return o

    def fill(o, c):
        run("v", [o], [], lambda e: e.memset(ap(o), c))
        return o

    def minus_total(o, i):
        run("v", [o], [i], lambda e: e.tensor_reduce(ap(o), ap(i), AX, ADD, negate=True))
        return o

    def gather(o, win, off, q="v"):
        if q == "v":
            run("v", [o], [win, off], lambda e: e.tensor_copy(ap(o), ap(win).indirect(ap(off))))
        else:
            run("s", [o], [win, off], lambda e: e.activation(ap(o), ap(win).indirect(ap(off)), AF.Copy))
        return o

    def act(o, i, func, scale=1.0, bias=0.0):
        ins = [i]
        a, b = sc(scale, ins), sc(bias, ins)
        run("s", [o], ins, lambda e: e.activation(ap(o), ap(i), func, bias=b, scale=a))
        return o

    def iota(o, pattern, base=0, lane=0):
        run("g", [o], [], lambda e: e.iota(ap(o), pattern, base, lane, allow_small_or_imprecise_dtypes=o[0] != "aI"))
        return o

    def const(o, c):
        return iota(o, [[0, o[2] - o[1]]], c)

    def asel(o, i, pattern, op, c, base):
        run("g", [o], [i], lambda e: e.affine_select(ap(o), ap(i), pattern, op, c, base, 0))
        return o

    def dma(q, o, i, sem):
        run(q, [v for v in (o,) if isinstance(v, tuple)], [v for v in (i,) if isinstance(v, tuple)],
            lambda e: e.dma_start(ap(o) if isinstance(o, tuple) else o, ap(i) if isinstance(i, tuple) else i), sem, 16)

    def quant(n, a, b, t, c):
        q, s, i = V(n + "q", a, b), V(n + "s", a, b), V(t, c, c + 4 * (b - a))
        run("v", [q, s], [i], lambda e: e.quantize_mx(ap(q), ap(s), ap(i)))

    def pickc(cq, wq, off):
        run("v", [cq], [wq, off], lambda e: e.tensor_copy(ap(cq).bitcast(dt.uint32), ap(wq).bitcast(dt.uint32).indirect(ap(off))))

    def mm(o, wq, ws, xq, xs, start, stop):
        run("t", [o] if start else [], [wq, ws, xq, xs], lambda e: e.matmul_mx(ap(o), ap(wq), ap(ws), ap(xq), ap(xs), start, stop))
        if not start:
            note(o, True, "t", "qt", count["qt"], dict(known["t"]))

    def send(pairs, width, bits, rsem, lsem, ins, arrive):
        sync("g", [], ins)
        xs = []
        for k, (d, src, dst) in enumerate(pairs):
            to = T.cores[d]
            rid, pid, _ = topo.addr(to)
            a, b = ap(src), ap(dst)
            if bits:
                a, b = a.bitcast(dt.uint8), b.bitcast(dt.uint8)
            mask = sum(1 << e for e in topo.engines(core, to)[width * k:width * k + width])
            xs.append(RemoteDMATransfer(dst_ids=[DstId(rid=rid, pnc=pid)], dma_engine_mask=mask,
                                        remote_sem=T.sem[rsem], src=a, dst=b))
        g.remote_dma_fused(xs, local_sem=T.sem[lsem])
        count[lsem] = count.get(lsem, 0) + width * len(xs)
        count[rsem] = count.get(rsem, 0) + arrive

    F1 = lambda: new("aF", 1)
    turn = 1 if r % 2 == 0 else -1
    order = [d for b in range(0, N, 2) for d in ((r + b) % N, (r + b) % N + turn)]
    others = order[1:]

    dma("y", V("uc", 0, 8), T.u[:, 0:8], "du")
    dma("s", V("zt", 64, 128), T.x[:, 960:1024], "de1")
    dma("y", V("zt", 0, 64), T.x[:, 0:64], "de0")
    dma("s", V("xt", 64, 576), T.x[:, 0:512], "dx0")
    dma("y", V("xt", 576, 1088), T.x[:, 512:1024], "dx1")

    lane = iota(new("aI", 1), [[0, 1]], 0, 1)
    jj = iota(new("aH", 64), [[0, 4], [1, 16]])
    ones = fill(new("aH", 128), 1.0)
    bI = ts(new("aI", 1), lane, 31, A.bitwise_and)
    bm = ts(F1(), bI, -15.5, ADD)
    w = act(F1(), bm, AF.Abs)
    half = act(new("aF", 16), sub(ones, 0, 16), AF.Copy, 1.0 / 36)
    fill(V("zt", 128, 640), 0.0)
    first = ts(F1(), w, 15.0, GE, -0.0625, MUL)
    q0 = ts(F1(), w, 15.9375, MUL, 0.0625 - 15.9375 * 15.5, ADD)
    cut = tt(F1(), first, q0, ADD)
    ft = new("aH", 256)
    f1 = ts(new("aH", 64), jj, 15.9375, MUL, cut, ADD)
    ts(sub(ft, 0, 64), f1, 0.0, MAX, 16.0, MIN)
    eq = scan(new("aF", 16), sub(ft, 0, 16), half)
    nrm = F1()

    halo = [(k, a, b) for k, a, b in ((r + 1, 16, 0), (r - 1, 0, 272)) if 0 <= k < N]
    wide = lambda k: 8 // sum(0 <= j < N for j in (k - 1, k + 1))
    quant("e", 0, 128, "zt", 0)
    for n, bits, rsem in (("q", True, "rhc"), ("s", False, "rhs")):
        at = lambda m, a: V(m + n, a, a + 16)
        send([(k, at("e", a), at("gr", b)) for k, a, b in halo], wide(r), bits, rsem, "lhalo",
             [at("e", a) for k, a, b in halo], sum(wide(k) for k, a, b in halo))
        for k, a, b in halo:
            note(at("gr", 0 if k < r else 272), True, None, rsem, count[rsem], {})
    t_e = iota(new("aF", 2), [[2, 2]], 1)
    t_y = const(new("aF", 2), 16 * r)
    t_l = iota(new("aF", 3), [[16, 3]], -1)
    t_d = new("aF", 8)
    nb = (N - r + 1) // 2
    iota(sub(t_d, 0, 2 * nb), [[-16, nb], [0, 2]], 383 - 8 * r)
    if nb < 4:
        iota(sub(t_d, 2 * nb, 8), [[-16, 4 - nb], [0, 2]], 383 - 8 * ((r + 2 * nb) % N))

    for t in (1, 2, 3):
        act(V("ut", t, 512, 4), ones, AF.Identity, 0.0, V("uc", t, t + 1))
    ts(V("ut", 0, 512, 4), ones, V("uc", 0, 1), MUL)
    for a in (64, 128, 192):
        act(sub(ft, a, a + 64), sub(ft, 0, 64), AF.Copy)
    if r == 0:
        fill(V("xt", 0, 64), 0.0)
    sgn, cells = new("aH", 256), new("aH", 256)
    for h in (0, 1):
        a = 0 if r == 0 and h == 0 else 16 + 128 * h
        quant("gr", a, 144 + 128 * h, "xt", 4 * a)
        if h == 0:
            quant("u", 0, 128, "ut", 0)
        a = 16 + 128 * h
        mm(V("ps", 512 * h, 512 * h + 128), V("uq", 0, 128), V("us", 0, 128), V("grq", a, a + 128), V("grs", a, a + 128), True, True)
    run("v", [nrm], [sub(eq, 15, 16)], lambda e: e.reciprocal(ap(nrm), ap(sub(eq, 15, 16))))
    for h in (0, 1):
        ts(sub(sgn, 128 * h, 128 * h + 128), V("ps", 512 * h, 512 * h + 128), 0.0, A.is_gt, -0.5, ADD)
    scan(cells, ft, sgn)
    own = V("sg", 16 * r, 16 * r + 16)
    ts(own, sub(cells, 15, 256, 16), nrm, MUL)
    send([(k, own, own) for k in others], 1, False, "rsign", "lsign", [own], N - 1)
    for k in others:
        note(V("sg", 16 * k, 16 * k + 16), True, None, "rsign", count["rsign"], {})
    g.sync.wait_ge(T.sem["lsign"], count["lsign"])
    known["y"]["lsign"] = count["lsign"]
    for k, (a, b) in enumerate(((0, 2048), (2048, 4096), (4096, 5120))):
        dma("y", V("wt", a, b), T.w[:, a:b], "dw%d" % k)

    t_tr = iota(new("aF", 16), [[1, 16]], (1 << 20) - 256)
    base = iota(new("aH", 256), [[-1, 16], [16, 16]], 31 - MID)
    onef = const(new("aF", 32), 1)
    rs = asel(new("aF", 32), asel(new("aF", 32), onef, [[1, 32]], NE, 0.0, 0), [[1, 32]], NE, -1.0, -16)
    win = const(new("aH", 384), MID)
    XS = const(new("aH", 32), 1000)
    npt = new("aF", 256)
    for a in range(8):
        iota(sub(npt, 32 * a, 32 * a + 32), [[0, 2], [128, 2], [2, 8]], 256 * a + 16 * r + 3)
    r32 = asel(new("aH", 256), const(new("aH", 256), 1), [[0, 8], [1, 32]], NE, 0.0, 0)

    alpha = act(new("aH", 128), ones, AF.Copy, scale=1.0 / 32)
    lo = ts(F1(), bm, 0.0, LT)
    one0 = ts(F1(), bm, -15.5, EQ)
    iF = ts(F1(), ts(new("aI", 1), lane, 15, A.bitwise_and), 0.0, ADD)
    d0 = act(new("aH", 128), ones, AF.Copy, scale=lo)
    hb = act(F1(), bm, AF.Identity, 0.5 * turn, 7.75 * turn)
    s1 = act(F1(), iF, AF.Identity, 1.0 - 0.5 * turn, hb)
    off_y = ts(new("aU", 2), t_y, iF, ADD)
    high = ts(F1(), iF, 8.0, GE, 56.0, MUL)
    la = ts(new("aF", 3), t_l, iF, ADD, 39.0, MIN)
    lb = ts(new("aI", 3), la, 0.2, MUL, -0.4, ADD)
    e13 = ts(new("aF", 2), t_e, iF, EQ)
    n13 = ts(new("aF", 2), t_e, iF, NE)
    lc = ts(new("aF", 3), lb, 11.0, MUL)
    off_d = ts(new("aU", 8), t_d, s1, SUB, high, SUB)
    ld = tt(new("aF", 3), lc, la, ADD)
    off_l = ts(new("aU", 3), ld, 0.0, MAX)
    quant("gr", 288 if r < N - 1 else 272, 416 if r < N - 1 else 400, "zt", 128)
    quant("la", SL * N + 16, LW, "zt", 128)
    i16 = act(F1(), iF, AF.Copy, scale=16.0)
    trash = act(new("aF", 16), t_tr, AF.Identity, bias=i16)
    sx = act(F1(), iF, AF.Identity, bias=-2.0)
    sx2 = act(F1(), sx, AF.Square)
    delta = act(F1(), act(F1(), sx2, AF.Identity, 7.0 / 3, -4.0 / 3), AF.Copy, scale=sx)
    z1 = act(F1(), sub(e13, 0, 1), AF.Identity, float(MID + 1), delta)
    z3 = act(F1(), sub(e13, 1, 2), AF.Identity, float(MID - 1), delta)
    val = new("aH", 256)
    act(sub(val, 16, 240), sub(base, 16, 240), AF.Identity, 1.0, delta)
    act(sub(val, 0, 16), sub(base, 0, 16), AF.Identity, sub(n13, 1, 2), z3)
    act(sub(val, 240, 256), sub(base, 240, 256), AF.Identity, sub(n13, 0, 1), z1)

    SV, X = new("aH", 128), new("aH", 128)
    sg = V("sg", 0, 128)
    act(sub(SV, 0, 127), sub(sg, 1, 128), AF.Sign)
    st = scan(new("aH", 128), alpha, sg, sub(sg, 0, 1))
    ts(sub(SV, 127, 128), sub(sg, 127, 128), -1.0, MAX, 1.0, MIN)
    pr = tt(new("aH", 128), st, SV, MUL)
    av = ts(new("aH", 128), pr, 18.0, LT)
    scan(X, d0, av, one0)

    Y = gather(new("aH", 32), X, off_y)
    act(sub(XS, 0, 8), sub(X, 15, 128, 16), AF.Copy)
    lbk = [act(F1(), iF, AF.Identity, bias=16.0 + 16 * k + 16 * SL) for k in range(5)]
    YT = tr(new("aH", 32), Y)
    S6 = scan(new("aF", 32), rs, YT)
    V6 = tt(new("aI", 16), sub(S6, 16, 32), sub(YT, 16, 32), MUL)
    A6 = ts(new("aI", 16), V6, 127 | 1 << 20, A.bitwise_and)
    o6 = tt(new("aF", 16), A6, trash, MAX)
    off = ts(new("aU", 16), o6, float((1 << 20) - 256), SUB)
    run("v", [win], [off, val], lambda e: e.tensor_copy(ap(win).indirect(ap(off)), ap(val)))
    D = gather(new("aH", 128), win, off_d)
    DT = tr(new("aH", 128), D)
    lw = new("aU", 48)
    run("v", [lw], [DT, off_l], lambda e: e.tensor_scalar(ap(lw), ap(DT).indirect(ap(off_l)), float(MID), None, ADD))

    gq, gs = V("grq", 0, 304), V("grs", 0, 304)
    home = lambda n, k: V(n, SL * k + 16, SL * k + SL)
    slot = lambda n, i: V(n, NC * i, NC * i + NC)
    for a, b in ((4, 7), (0, 4)):
        pickc(V("slq", NC * a, NC * b), gq, sub(lw, 6 + 5 * a, 6 + 5 * b))
        gather(V("sls", NC * a, NC * b), gs, sub(lw, 6 + 5 * a, 6 + 5 * b), "s")
    for n, bits, m, a, b, width in (("q", True, "rlc", 4, 7, 2), ("q", True, "rlc", 0, 4, 2), ("s", False, "rls", 0, 7, 1)):
        send([(others[i], slot("sl" + n, i), home("la" + n, r)) for i in range(a, b)], width, bits, m, "lland",
             [slot("sl" + n, i) for i in range(a, b)], width * (N - 1) if a == 0 else 0)
        if a == 0:
            for k in others:
                note(home("la" + n, k), True, None, m, count[m], {})

    XT = tr(new("aH", 32), XS)
    C = minus_total(F1(), sub(XT, 0, 16))
    ind = act(new("aH", 256), npt, AF.Sign, 0.5, C)
    pickc(V("laq", SL * r, SL * r + SL), gq, sub(lw, 0, 6))
    gather(V("las", SL * r, SL * r + SL), gs, sub(lw, 0, 6), "s")
    quant("w", 0, 512, "wt", 0)
    it = tr(new("aH", 256), ind)
    iq = scan(new("aH", 256), r32, it)
    lf, lu = new("aF", 40), new("aU", 40)
    for k in range(5):
        act(sub(lf, 8 * k, 8 * k + 8), sub(iq, 31, 256, 32), AF.Identity, SL / 2.0, lbk[k])
    for a, b in ((512, 1024), (1024, 1280)):
        quant("w", a, b, "wt", 4 * a)
    ts(lu, lf, 0.0, ADD)

    tk = lambda n, k: V(n, 128 * k, 128 * k + 128)
    lk = lambda k: sub(lu, 8 * k, 8 * k + 8)
    for k in range(5):
        pickc(tk("tq", k), V("laq", 0, LW), lk(k))
    for k in range(5):
        gather(tk("ts", k), V("las", 0, LW), lk(k), "ssvsv"[k])
    for k in range(5):
        for o in (0, 1):
            a = 128 * (2 * KW[k] + o)
            mm(V("ps", 1024 + 512 * o, 1152 + 512 * o), V("wq", a, a + 128), V("ws", a, a + 128), tk("tq", k), tk("ts", k), k == 0, k == 4)
    cp(V("yo", 0, 128), V("ps", 1024, 1152))
    act(V("yo", 128, 256), V("ps", 1536, 1664), AF.Copy)
    dma("y", T.y[:, 0:128], V("yo", 0, 128), "dy0")
    dma("s", T.y[:, 128:256], V("yo", 128, 256), "dy1")
    for sem in SEMAPHORES:
        if count.get(sem, 0) > known["g"].get(sem, 0):
            g.wait_ge(T.sem[sem], count[sem])
